import numpy as np
import ml_dtypes


def mxq(x, axis, fmt="e4m3"):
    dtype, down = {"e4m3": (ml_dtypes.float8_e4m3fn, 7), "e5m2": (ml_dtypes.float8_e5m2, 14)}[fmt]
    v = np.moveaxis(np.asarray(x, np.float32).astype(ml_dtypes.bfloat16).astype(np.float64), axis, -1)
    blocks = v.reshape(v.shape[:-1] + (-1, 32))
    amax = np.abs(blocks).max(-1, keepdims=True)
    byte = np.maximum(np.where(amax > 0, np.frexp(amax)[1] - 1 + 127, 0) - down, 1)
    scale = np.exp2(byte - 127.0)
    codes = (blocks / scale).astype(np.float32).astype(dtype).astype(np.float64)
    return np.moveaxis((codes * scale).reshape(v.shape), -1, axis)


WIDE = False


def mx_kscale(k):
    if not WIDE:
        return np.ones(k)
    levels = np.array([10, -10, 5, -5, 0])
    if k % 512:
        return np.exp2(np.random.permutation(np.resize(levels, k // 32))).repeat(32)
    a = np.empty((k // 512, 16))
    for p in range(k // 512):
        a[p, :8] = np.random.permutation(np.resize(levels, 8))
        for g in range(8):
            far = levels[np.abs(levels - a[p, g]) >= 10]
            a[p, g + 8] = far[np.random.randint(len(far))]
    return np.exp2(a.ravel()).repeat(32)


def f64(x):
    return np.asarray(x).astype(np.float64)


def striped(idx):
    return np.tile(idx.reshape(-1, 16).T, (8, 1)).astype(np.uint16)


def unstriped(offs):
    return offs[:16].T.reshape(-1).astype(np.int64)


def relu(v):
    return np.maximum(v, 0.0)


def gelu(v):
    return 0.5 * v * (1.0 + np.tanh(np.sqrt(2.0 / np.pi) * (v + 0.044715 * v**3)))


K, T, S, D, V, H, N, U = 1024, 2048, 1024, 2, 512, 512, 256, 256
P = 2 ** 7


def setup_inputs():
    n = np.random.standard_normal
    s = mx_kscale(K)[:, None]
    u = mx_kscale(H)
    return {
        "xT": (n((K, T)) * s).astype(np.float32),
        "w1": (n((K, H)) / np.sqrt(K) / s * u).astype(np.float32),
        "w2": (n((H, N)) / np.sqrt(H) / u[:, None]).astype(np.float32),
        "gate": (np.tile(np.random.uniform(0.2, 1.0, (D, 1, V)) / np.sqrt(D), (1, P, 1))).astype(np.float32),
        "gate2": (np.tile(np.random.uniform(0.2, 1.0, (D, 1, U)) / np.sqrt(D), (1, P, 1))).astype(np.float32),
        "offs": striped(np.random.permutation(T)[:S]),
        "pos1": striped(np.random.permutation(S)[:V]),
        "pos2": striped(np.random.permutation(S)[:V]),
        "nxt1": striped(np.random.permutation(V)[:U]),
        "nxt2": striped(np.random.permutation(V)[:U]),
    }


def reference(xT, w1, w2, gate, gate2, offs, pos1, pos2, nxt1, nxt2):
    xq = mxq(f64(xT)[:, unstriped(offs)], 0, "e4m3")
    h = gelu(mxq(f64(w1), 0, "e4m3").T @ xq)
    z = h[:, unstriped(pos1)] * f64(gate)[0, :1] + h[:, unstriped(pos2)] * f64(gate)[1, :1]
    g = relu(mxq(f64(w2), 0, "e4m3").T @ mxq(z, 0, "e4m3"))
    return g[:, unstriped(nxt1)] * f64(gate2)[0, :1] + g[:, unstriped(nxt2)] * f64(gate2)[1, :1]

@@ -1,0 +1,240 @@
+from contextlib import ExitStack
+
+import concourse.mybir as mybir
+
+K, T, S, V, H, N, U = 1024, 2048, 1024, 512, 512, 256, 256
+FLOPS = 2 * K * H * S + 2 * H * N * V
+
+F32 = mybir.dt.float32
+BF16 = mybir.dt.bfloat16
+U32 = mybir.dt.uint32
+I32 = mybir.dt.int32
+U16 = mybir.dt.uint16
+U8 = mybir.dt.uint8
+FP8X4 = mybir.dt.float8_e4m3fn_x4
+ACT = mybir.ActivationFunctionType
+MULT = mybir.AluOpType.mult
+ADD = mybir.AluOpType.add
+
+P = 128
+PACK = 4
+K_PASS = P * PACK
+PASSES = K // K_PASS
+BANK = 512
+X_CHUNKS = [[512, 512, 512, 512], [512, 512, 512, 256, 256]]
+VECTOR_NODES = 128
+W1_CHUNK = 256
+V_SLICES = [(0, 384), (384, 512)]
+Z_SPANS = [[(0, 256), (256, 384)], [(384, 512)]]
+
+
+def interleave_views(dst, src):
+    return (dst.rearrange("p (c i) j -> p c j i", i=4), src.rearrange("p j (c i) -> p c j i", i=4))
+
+
+def tile_picked_hop2_gelu_e_kernel(tc, xT, w1, w2, gate, gate2, offs, pos1, pos2, nxt1, nxt2, out):
+    nc = tc.nc
+    with ExitStack() as ctx:
+        keep = ctx.enter_context(tc.tile_pool(name="keep", bufs=1))
+        psum = ctx.enter_context(tc.psum_pool(name="psum", bufs=1))
+
+        def load_list(name, src):
+            tile = keep.tile(list(src.shape), U16, name=name)
+            nc.sync.dma_start(tile[:], src)
+            return tile
+
+        warm = keep.tile([P, 2], F32, name="warm")
+        nc.vector.memset(warm[:, 0:1], 0.0)
+        nc.scalar.activation(warm[:, 1:2], warm[:, 0:1], ACT.Gelu_apprx_tanh)
+
+        x_scales = keep.tile([P, T], U8, name="x_scales", align_bytes=64)
+        nc.vector.memset(x_scales[:].bitcast(I32), 0)
+        x_words = [keep.tile([P, T], U32, name=f"x_words{g}", align_bytes=64) for g in range(PASSES)]
+
+        x_raw = {}
+        lists = {}
+        for g in range(PASSES):
+            c0 = 0
+            for width in X_CHUNKS[g]:
+                raw = keep.tile([P, PACK, width], F32, name=f"x_raw{g}_{c0}")
+                rows = xT[g * K_PASS : (g + 1) * K_PASS, c0 : c0 + width]
+                nc.sync.dma_start(raw[:], rows.rearrange("(p j) c -> p j c", j=PACK))
+                x_raw[g, c0] = raw
+                c0 = c0 + width
+                if g == 0 and c0 == 1024:
+                    lists["offs"] = load_list("offs", offs)
+                    lists["pos1"] = load_list("pos1", pos1)
+                    lists["pos2"] = load_list("pos2", pos2)
+        w1_raw = {}
+        for g in range(PASSES):
+            for c0 in range(0, H, W1_CHUNK):
+                raw = keep.tile([P, PACK, W1_CHUNK], F32, name=f"w1_raw{g}_{c0}")
+                rows = w1[g * K_PASS : (g + 1) * K_PASS, c0 : c0 + W1_CHUNK]
+                nc.sync.dma_start(raw[:], rows.rearrange("(p j) c -> p j c", j=PACK))
+                w1_raw[g, c0] = raw
+        gate_sb = keep.tile([P, 2, V], F32, name="gate_sb")
+        nc.sync.dma_start(gate_sb[:], gate.rearrange("d p v -> p d v"))
+        w2_raw = keep.tile([P, PACK, N], F32, name="w2_raw")
+        nc.sync.dma_start(w2_raw[:], w2.rearrange("(p j) c -> p j c", j=PACK))
+        gate2_sb = keep.tile([P, 2, U], F32, name="gate2_sb")
+        nc.sync.dma_start(gate2_sb[:], gate2.rearrange("d p v -> p d v"))
+        lists["nxt1"] = load_list("nxt1", nxt1)
+        lists["nxt2"] = load_list("nxt2", nxt2)
+
+        halves = range(S // BANK)
+        picked_words = {}
+
+        def gather_words(g, half):
+            tile = keep.tile([P, BANK], U32, name=f"picked_words{g}_{half}", align_bytes=64)
+            cols = slice(half * BANK // 16, (half + 1) * BANK // 16)
+            nc.vector.tensor_copy(tile[:], x_words[g][:].indirect(lists["offs"][:, cols]))
+            picked_words[g, half] = tile
+
+        for g in range(PASSES):
+            c0 = 0
+            for n, width in enumerate(X_CHUNKS[g]):
+                raw = x_raw[g, c0]
+                grouped = keep.tile([P, width, PACK], BF16, name=f"x_bf{g}_{c0}", align_bytes=64)
+                cut = width - VECTOR_NODES
+                dst, src = interleave_views(grouped[:, :cut, :], raw[:, :, :cut])
+                nc.scalar.activation(dst, src, ACT.Copy)
+                dst, src = interleave_views(grouped[:, cut:, :], raw[:, :, cut:])
+                nc.vector.tensor_copy(dst, src)
+                if g == 1 and n < 2:
+                    gather_words(0, n)
+                nc.vector.quantize_mx(
+                    out=x_words[g][:, c0 : c0 + width].bitcast(FP8X4),
+                    scales=x_scales[4 * g :, c0 : c0 + width],
+                    in_=grouped[:].rearrange("p c j -> p (c j)"),
+                )
+                c0 = c0 + width
+        picked_scales = keep.tile([P, S], U8, name="picked_scales", align_bytes=64)
+        nc.vector.tensor_copy(picked_scales[:], x_scales[:].indirect(lists["offs"][:]))
+
+        w1_words, w1_scales, w1_bf = [], [], []
+        for g in range(PASSES):
+            grouped = keep.tile([P, PACK, P, PACK], BF16, name=f"w1_bf{g}", align_bytes=64)
+            for c0 in range(0, H, W1_CHUNK):
+                m0, m1 = c0 // PACK, (c0 + W1_CHUNK) // PACK
+                nc.scalar.activation(
+                    grouped[:, :, m0:m1, :].rearrange("p t m j -> p m j t"),
+                    w1_raw[g, c0][:].rearrange("p j (m t) -> p m j t", t=PACK),
+                    ACT.Copy,
+                )
+            w1_bf.append(grouped)
+            w1_words.append(keep.tile([P, H], U32, name=f"w1_words{g}", align_bytes=64))
+            w1_scales.append(keep.tile([P, H], U8, name=f"w1_scales{g}", align_bytes=64))
+
+        def quantize_w1(g, t0, t1):
+            nc.vector.quantize_mx(
+                out=w1_words[g][:, t0 * P : t1 * P].bitcast(FP8X4),
+                scales=w1_scales[g][:, t0 * P : t1 * P],
+                in_=w1_bf[g][:, t0:t1].rearrange("p t m j -> p (t m j)"),
+            )
+
+        acc = {}
+
+        def first_product(g, t, half):
+            if g == 0:
+                acc[t, half] = psum.tile([P, BANK], F32, name=f"acc{t}_{half}", tag=f"bank{2 * t + half}")
+            nc.tensor.matmul_mx(
+                out=acc[t, half][:],
+                lhsT=w1_words[g][:, t * P : (t + 1) * P].bitcast(FP8X4),
+                lhsT_scale=w1_scales[g][:, t * P : (t + 1) * P],
+                rhs=picked_words[g, half][:].bitcast(FP8X4),
+                rhs_scale=picked_scales[4 * g :, half * BANK : (half + 1) * BANK],
+                start=(g == 0),
+                stop=(g == PASSES - 1),
+            )
+
+        gather_words(1, 0)
+        quantize_w1(0, 0, PACK)
+        gather_words(1, 1)
+        for t in range(PACK):
+            for half in halves:
+                first_product(0, t, half)
+        h = []
+        for t in range(PACK):
+            quantize_w1(1, t, t + 1)
+            h_t = keep.tile([P, S], F32, name=f"h{t}")
+            for half in halves:
+                first_product(1, t, half)
+                nc.scalar.activation(h_t[:, half * BANK : (half + 1) * BANK], acc[t, half][:], ACT.Gelu_apprx_tanh)
+            h.append(h_t)
+
+        w2_bf = keep.tile([P, N, PACK], BF16, name="w2_bf", align_bytes=64)
+        dst, src = interleave_views(w2_bf[:], w2_raw[:])
+        nc.scalar.activation(dst, src, ACT.Copy)
+        w2_words = keep.tile([P, N], U32, name="w2_words", align_bytes=64)
+        w2_scales = keep.tile([P, N], U8, name="w2_scales", align_bytes=64)
+
+        g_sb = [keep.tile([P, V], F32, name=f"g{b}") for b in range(N // P)]
+        terms = {}
+
+        def hop1_gathers(s):
+            v0, v1 = V_SLICES[s]
+            for d in range(2):
+                terms[s, d] = keep.tile([P, PACK, v1 - v0], F32, name=f"term{s}_{d}")
+            for t in range(PACK):
+                for d, name in enumerate(("pos1", "pos2")):
+                    nc.vector.tensor_tensor(
+                        terms[s, d][:, t, :],
+                        h[t][:].indirect(lists[name][:, v0 // 16 : v1 // 16]),
+                        gate_sb[:, d, v0:v1],
+                        MULT,
+                    )
+
+        def hop1_sum(s):
+            v0, v1 = V_SLICES[s]
+            z = keep.tile([P, PACK, v1 - v0], F32, name=f"z{s}")
+            nc.vector.tensor_tensor(z[:], terms[s, 0][:], terms[s, 1][:], ADD)
+            z_bf = keep.tile([P, v1 - v0, PACK], BF16, name=f"z_bf{s}", align_bytes=64)
+            dst, src = interleave_views(z_bf[:], z[:])
+            if s == len(V_SLICES) - 1:
+                nc.vector.tensor_copy(dst, src)
+            else:
+                nc.scalar.activation(dst, src, ACT.Copy)
+            return z_bf
+
+        banks = [0]
+
+        def second_product(s, z_bf):
+            base = V_SLICES[s][0]
+            for v0, v1 in Z_SPANS[s]:
+                words = keep.tile([P, v1 - v0], U32, name=f"z_words{v0}", align_bytes=64)
+                scales = keep.tile([P, v1 - v0], U8, name=f"z_scales{v0}", align_bytes=64)
+                nc.vector.quantize_mx(
+                    out=words[:].bitcast(FP8X4),
+                    scales=scales[:],
+                    in_=z_bf[:, v0 - base : v1 - base, :].rearrange("p c j -> p (c j)"),
+                )
+                for b in range(N // P):
+                    bank = psum.tile([P, BANK], F32, name=f"g_acc{v0}_{b}", tag=f"bank{banks[0]}")
+                    banks[0] = banks[0] + 1
+                    nc.tensor.matmul_mx(
+                        out=bank[:, : v1 - v0],
+                        lhsT=w2_words[:, b * P : (b + 1) * P].bitcast(FP8X4),
+                        lhsT_scale=w2_scales[:, b * P : (b + 1) * P],
+                        rhs=words[:].bitcast(FP8X4),
+                        rhs_scale=scales[:],
+                        start=True,
+                        stop=True,
+                    )
+                    nc.scalar.activation(g_sb[b][:, v0:v1], bank[:, : v1 - v0], ACT.Relu)
+
+        hop1_gathers(0)
+        z_first = hop1_sum(0)
+        nc.vector.quantize_mx(
+            out=w2_words[:].bitcast(FP8X4), scales=w2_scales[:], in_=w2_bf[:].rearrange("p c j -> p (c j)")
+        )
+        hop1_gathers(1)
+        second_product(0, z_first)
+        second_product(1, hop1_sum(1))
+
+        for b in range(N // P):
+            pair = keep.tile([P, 2, U], F32, name=f"pair{b}")
+            for d, name in enumerate(("nxt1", "nxt2")):
+                nc.vector.tensor_tensor(pair[:, d, :], g_sb[b][:].indirect(lists[name][:]), gate2_sb[:, d, :], MULT)
+            result = keep.tile([P, U], F32, name=f"result{b}")
+            nc.vector.tensor_tensor(result[:], pair[:, 0, :], pair[:, 1, :], ADD)
+            nc.sync.dma_start(out[b * P : (b + 1) * P, :], result[:])

@@ -1,6 +1,7 @@
 from contextlib import ExitStack
 
 import concourse.mybir as mybir
+from concourse.masks import make_identity
 
 K, T, S, V, H, N, U = 1024, 2048, 1024, 512, 512, 256, 256
 FLOPS = 2 * K * H * S + 2 * H * N * V
@@ -22,7 +23,7 @@ K_PASS = P * PACK
 PASSES = K // K_PASS
 BANK = 512
 X_CHUNKS = [[512, 512, 512, 512], [512, 512, 512, 256, 256]]
-VECTOR_NODES = 128
+SCALAR_NODES = {512: 256, 256: 96}
 W1_CHUNK = 256
 V_SLICES = [(0, 384), (384, 512)]
 Z_SPANS = [[(0, 256), (256, 384)], [(384, 512)]]
@@ -46,10 +47,12 @@ def tile_picked_hop2_gelu_e_kernel(tc, xT, w1, w2, gate, gate2, offs, pos1, pos2
         warm = keep.tile([P, 2], F32, name="warm")
         nc.vector.memset(warm[:, 0:1], 0.0)
         nc.scalar.activation(warm[:, 1:2], warm[:, 0:1], ACT.Gelu_apprx_tanh)
+        ident = keep.tile([P, P], F32, name="ident")
+        make_identity(nc, ident[:])
 
         x_scales = keep.tile([P, T], U8, name="x_scales", align_bytes=64)
         nc.vector.memset(x_scales[:].bitcast(I32), 0)
-        x_words = [keep.tile([P, T], U32, name=f"x_words{g}", align_bytes=64) for g in range(PASSES)]
+        x_words = [keep.tile([P, T], U32, name=f"x_words{g}", tag=f"x_words{g}", align_bytes=64) for g in range(PASSES)]
 
         x_raw = {}
         lists = {}
@@ -66,14 +69,19 @@ def tile_picked_hop2_gelu_e_kernel(tc, xT, w1, w2, gate, gate2, offs, pos1, pos2
                     lists["pos1"] = load_list("pos1", pos1)
                     lists["pos2"] = load_list("pos2", pos2)
         w1_raw = {}
-        for g in range(PASSES):
-            for c0 in range(0, H, W1_CHUNK):
+        for c0 in range(0, H, W1_CHUNK):
+            for g in range(PASSES):
                 raw = keep.tile([P, PACK, W1_CHUNK], F32, name=f"w1_raw{g}_{c0}")
                 rows = w1[g * K_PASS : (g + 1) * K_PASS, c0 : c0 + W1_CHUNK]
                 nc.sync.dma_start(raw[:], rows.rearrange("(p j) c -> p j c", j=PACK))
                 w1_raw[g, c0] = raw
-        gate_sb = keep.tile([P, 2, V], F32, name="gate_sb")
-        nc.sync.dma_start(gate_sb[:], gate.rearrange("d p v -> p d v"))
+        split = V_SLICES[0][1]
+        gates = {}
+        for d in range(2):
+            gates[0, d] = keep.tile([P, split], F32, name=f"gate_first{d}", tag=f"gate{d}")[:]
+            nc.sync.dma_start(gates[0, d], gate[d, :, :split])
+        gate_rest = keep.tile([P, 2, V - split], F32, name="gate_rest")
+        nc.sync.dma_start(gate_rest[:], gate[:, :, split:].rearrange("d p v -> p d v"))
         w2_raw = keep.tile([P, PACK, N], F32, name="w2_raw")
         nc.sync.dma_start(w2_raw[:], w2.rearrange("(p j) c -> p j c", j=PACK))
         gate2_sb = keep.tile([P, 2, U], F32, name="gate2_sb")
@@ -83,133 +91,147 @@ def tile_picked_hop2_gelu_e_kernel(tc, xT, w1, w2, gate, gate2, offs, pos1, pos2
 
         halves = range(S // BANK)
         picked_words = {}
+        picked_scales = {}
 
-        def gather_words(g, half):
-            tile = keep.tile([P, BANK], U32, name=f"picked_words{g}_{half}", align_bytes=64)
-            cols = slice(half * BANK // 16, (half + 1) * BANK // 16)
-            nc.vector.tensor_copy(tile[:], x_words[g][:].indirect(lists["offs"][:, cols]))
+        def offs_half(half):
+            return lists["offs"][:, half * BANK // 16 : (half + 1) * BANK // 16]
+
+        def gather_words(g, half, tag, pieces=1):
+            tile = keep.tile([P, BANK], U32, name=f"picked_words{g}_{half}", tag=tag, align_bytes=64)
+            step = BANK // pieces
+            for e0 in range(0, BANK, step):
+                entries = offs_half(half)[:, e0 // 16 : (e0 + step) // 16]
+                nc.vector.tensor_copy(tile[:, e0 : e0 + step], x_words[g][:].indirect(entries))
             picked_words[g, half] = tile
+
+        def gather_scales(half, tag):
+            tile = keep.tile([P, BANK], U8, name=f"picked_scales{half}", tag=tag, align_bytes=64)
+            nc.vector.tensor_copy(tile[:], x_scales[:].indirect(offs_half(half)))
+            picked_scales[half] = tile
 
         for g in range(PASSES):
             c0 = 0
             for n, width in enumerate(X_CHUNKS[g]):
                 raw = x_raw[g, c0]
                 grouped = keep.tile([P, width, PACK], BF16, name=f"x_bf{g}_{c0}", align_bytes=64)
-                cut = width - VECTOR_NODES
+                cut = SCALAR_NODES[width]
                 dst, src = interleave_views(grouped[:, :cut, :], raw[:, :, :cut])
                 nc.scalar.activation(dst, src, ACT.Copy)
                 dst, src = interleave_views(grouped[:, cut:, :], raw[:, :, cut:])
                 nc.vector.tensor_copy(dst, src)
                 if g == 1 and n < 2:
-                    gather_words(0, n)
+                    gather_words(0, n, f"words0_{n}")
                 nc.vector.quantize_mx(
                     out=x_words[g][:, c0 : c0 + width].bitcast(FP8X4),
                     scales=x_scales[4 * g :, c0 : c0 + width],
                     in_=grouped[:].rearrange("p c j -> p (c j)"),
                 )
                 c0 = c0 + width
-        picked_scales = keep.tile([P, S], U8, name="picked_scales", align_bytes=64)
-        nc.vector.tensor_copy(picked_scales[:], x_scales[:].indirect(lists["offs"][:]))
 
-        w1_words, w1_scales, w1_bf = [], [], []
-        for g in range(PASSES):
-            grouped = keep.tile([P, PACK, P, PACK], BF16, name=f"w1_bf{g}", align_bytes=64)
-            for c0 in range(0, H, W1_CHUNK):
-                m0, m1 = c0 // PACK, (c0 + W1_CHUNK) // PACK
-                nc.scalar.activation(
-                    grouped[:, :, m0:m1, :].rearrange("p t m j -> p m j t"),
-                    w1_raw[g, c0][:].rearrange("p j (m t) -> p m j t", t=PACK),
-                    ACT.Copy,
-                )
-            w1_bf.append(grouped)
-            w1_words.append(keep.tile([P, H], U32, name=f"w1_words{g}", align_bytes=64))
-            w1_scales.append(keep.tile([P, H], U8, name=f"w1_scales{g}", align_bytes=64))
+        w1_words, w1_scales = {}, {}
 
-        def quantize_w1(g, t0, t1):
+        def quantize_w1(g, c, words):
+            c0, m0 = c * P // W1_CHUNK * W1_CHUNK, c * P % W1_CHUNK
+            grouped = keep.tile([P, P, PACK], BF16, name=f"w1_bf{g}_{c}", tag=f"w1_bf{g}_{c}", align_bytes=64)
+            dst, src = interleave_views(grouped[:], w1_raw[g, c0][:, :, m0 : m0 + P])
+            nc.scalar.activation(dst, src, ACT.Copy)
+            w1_words[g, c] = words
+            w1_scales[g, c] = keep.tile([P, P], U8, name=f"w1_scales{g}_{c}", align_bytes=64)
             nc.vector.quantize_mx(
-                out=w1_words[g][:, t0 * P : t1 * P].bitcast(FP8X4),
-                scales=w1_scales[g][:, t0 * P : t1 * P],
-                in_=w1_bf[g][:, t0:t1].rearrange("p t m j -> p (t m j)"),
+                out=words.bitcast(FP8X4), scales=w1_scales[g, c][:], in_=grouped[:].rearrange("p c j -> p (c j)")
             )
 
-        acc = {}
+        first_words = keep.tile([P, PASSES, P], U32, name="w1_first", align_bytes=64)
+        gather_scales(0, "scales0")
+        gather_words(1, 0, "words1_0")
+        quantize_w1(0, 0, first_words[:, 0, :])
+        quantize_w1(1, 0, first_words[:, 1, :])
+        gather_scales(1, "w1_bf0_0")
+        gather_words(1, 1, "w1_bf1_0", 2)
+        later_words = keep.tile([P, PASSES, H - P], U32, name="w1_later", tag="x_words1", align_bytes=64)
+        for c in range(1, H // P):
+            for g in range(PASSES):
+                quantize_w1(g, c, later_words[:, g, (c - 1) * P : c * P])
 
-        def first_product(g, t, half):
-            if g == 0:
-                acc[t, half] = psum.tile([P, BANK], F32, name=f"acc{t}_{half}", tag=f"bank{2 * t + half}")
-            nc.tensor.matmul_mx(
-                out=acc[t, half][:],
-                lhsT=w1_words[g][:, t * P : (t + 1) * P].bitcast(FP8X4),
-                lhsT_scale=w1_scales[g][:, t * P : (t + 1) * P],
-                rhs=picked_words[g, half][:].bitcast(FP8X4),
-                rhs_scale=picked_scales[4 * g :, half * BANK : (half + 1) * BANK],
-                start=(g == 0),
-                stop=(g == PASSES - 1),
-            )
-
-        gather_words(1, 0)
-        quantize_w1(0, 0, PACK)
-        gather_words(1, 1)
-        for t in range(PACK):
-            for half in halves:
-                first_product(0, t, half)
         h = []
-        for t in range(PACK):
-            quantize_w1(1, t, t + 1)
-            h_t = keep.tile([P, S], F32, name=f"h{t}")
-            for half in halves:
-                first_product(1, t, half)
-                nc.scalar.activation(h_t[:, half * BANK : (half + 1) * BANK], acc[t, half][:], ACT.Gelu_apprx_tanh)
-            h.append(h_t)
-
-        w2_bf = keep.tile([P, N, PACK], BF16, name="w2_bf", align_bytes=64)
-        dst, src = interleave_views(w2_bf[:], w2_raw[:])
-        nc.scalar.activation(dst, src, ACT.Copy)
-        w2_words = keep.tile([P, N], U32, name="w2_words", align_bytes=64)
-        w2_scales = keep.tile([P, N], U8, name="w2_scales", align_bytes=64)
+        groups = 0
+        for c in range(H // P):
+            spans = [(0, 0, BANK), (1, 0, BANK // 2), (1, BANK // 2, BANK)] if c == 0 else [(0, 0, BANK), (1, 0, BANK)]
+            h_c = keep.tile([P, S], F32, name=f"h{c}")
+            for half, e0, e1 in spans:
+                acc = psum.tile([P, BANK], F32, name=f"acc{groups}", tag=f"bank{groups % 4}")
+                groups = groups + 1
+                for g in range(PASSES):
+                    nc.tensor.matmul_mx(
+                        out=acc[:, : e1 - e0],
+                        lhsT=w1_words[g, c].bitcast(FP8X4),
+                        lhsT_scale=w1_scales[g, c][:],
+                        rhs=picked_words[g, half][:, e0:e1].bitcast(FP8X4),
+                        rhs_scale=picked_scales[half][4 * g :, e0:e1],
+                        start=(g == 0),
+                        stop=(g == PASSES - 1),
+                    )
+                nc.scalar.activation(
+                    h_c[:, half * BANK + e0 : half * BANK + e1], acc[:, : e1 - e0], ACT.Gelu_apprx_tanh
+                )
+            h.append(h_c)
 
         g_sb = [keep.tile([P, V], F32, name=f"g{b}") for b in range(N // P)]
-        terms = {}
+        z_rows = {}
 
-        def hop1_gathers(s):
+        def hop1(s):
             v0, v1 = V_SLICES[s]
-            for d in range(2):
-                terms[s, d] = keep.tile([P, PACK, v1 - v0], F32, name=f"term{s}_{d}")
-            for t in range(PACK):
+            blocks = (v1 - v0) // P
+            z_rows[s] = keep.tile([P, blocks, 2, P, 2], BF16, name=f"z_rows{s}")
+            for c in range(H // P):
+                terms = keep.tile([P, 2, v1 - v0], F32, name=f"terms{s}_{c}")
                 for d, name in enumerate(("pos1", "pos2")):
                     nc.vector.tensor_tensor(
-                        terms[s, d][:, t, :],
-                        h[t][:].indirect(lists[name][:, v0 // 16 : v1 // 16]),
-                        gate_sb[:, d, v0:v1],
+                        terms[:, d, :],
+                        h[c][:].indirect(lists[name][:, v0 // 16 : v1 // 16]),
+                        gates[s, d],
                         MULT,
                     )
-
-        def hop1_sum(s):
-            v0, v1 = V_SLICES[s]
-            z = keep.tile([P, PACK, v1 - v0], F32, name=f"z{s}")
-            nc.vector.tensor_tensor(z[:], terms[s, 0][:], terms[s, 1][:], ADD)
-            z_bf = keep.tile([P, v1 - v0, PACK], BF16, name=f"z_bf{s}", align_bytes=64)
-            dst, src = interleave_views(z_bf[:], z[:])
-            if s == len(V_SLICES) - 1:
-                nc.vector.tensor_copy(dst, src)
-            else:
-                nc.scalar.activation(dst, src, ACT.Copy)
-            return z_bf
+                turned = psum.tile([P, blocks, P], F32, name=f"turned{s}_{c}", tag=f"bank{4 + c % 2}")
+                for vb in range(blocks):
+                    for d in range(2):
+                        nc.tensor.matmul(
+                            turned[:, vb, :],
+                            terms[:, d, vb * P : (vb + 1) * P],
+                            ident[:],
+                            start=(d == 0),
+                            stop=(d == 1),
+                            is_transpose=True,
+                        )
+                nc.scalar.copy(
+                    z_rows[s][:, :, :, 32 * c : 32 * (c + 1), :],
+                    turned[:].rearrange("v b (q u e) -> v b u q e", u=2, e=2),
+                )
 
         banks = [0]
 
-        def second_product(s, z_bf):
+        def second_product(s):
             base = V_SLICES[s][0]
+            row_words = z_rows[s][:].rearrange("v b u p e -> v (b u p e)").bitcast(F32)
             for v0, v1 in Z_SPANS[s]:
+                blocks = (v1 - v0) // P
+                back = psum.tile([P, blocks, 2, P], F32, name=f"back{v0}", tag=f"bank{6 + banks[0] // 2 % 2}")
+                for vb in range(blocks):
+                    for u in range(2):
+                        w0 = (((v0 - base) // P + vb) * 2 + u) * P
+                        nc.tensor.transpose(back[:, vb, u, :], row_words[:, w0 : w0 + P], ident[:])
+                z_bf = keep.tile([P, (v1 - v0) * PACK], BF16, name=f"z_bf{v0}", align_bytes=64)
+                dst = z_bf[:].bitcast(F32).rearrange("p (b v u) -> p b v u", u=2, v=P)
+                src = back[:].rearrange("p b u v -> p b v u")
+                if s == len(V_SLICES) - 1:
+                    nc.vector.tensor_copy(dst, src)
+                else:
+                    nc.scalar.copy(dst, src)
                 words = keep.tile([P, v1 - v0], U32, name=f"z_words{v0}", align_bytes=64)
                 scales = keep.tile([P, v1 - v0], U8, name=f"z_scales{v0}", align_bytes=64)
-                nc.vector.quantize_mx(
-                    out=words[:].bitcast(FP8X4),
-                    scales=scales[:],
-                    in_=z_bf[:, v0 - base : v1 - base, :].rearrange("p c j -> p (c j)"),
-                )
+                nc.vector.quantize_mx(out=words[:].bitcast(FP8X4), scales=scales[:], in_=z_bf[:])
                 for b in range(N // P):
-                    bank = psum.tile([P, BANK], F32, name=f"g_acc{v0}_{b}", tag=f"bank{banks[0]}")
+                    bank = psum.tile([P, BANK], F32, name=f"g_acc{v0}_{b}", tag=f"bank{banks[0] % 4}")
                     banks[0] = banks[0] + 1
                     nc.tensor.matmul_mx(
                         out=bank[:, : v1 - v0],
@@ -222,14 +244,22 @@ def tile_picked_hop2_gelu_e_kernel(tc, xT, w1, w2, gate, gate2, offs, pos1, pos2
                     )
                     nc.scalar.activation(g_sb[b][:, v0:v1], bank[:, : v1 - v0], ACT.Relu)
 
-        hop1_gathers(0)
-        z_first = hop1_sum(0)
+        hop1(0)
+        w2_bf = keep.tile([P, N, PACK], BF16, name="w2_bf", tag="words0_1", align_bytes=64)
+        dst, src = interleave_views(w2_bf[:], w2_raw[:])
+        nc.scalar.activation(dst, src, ACT.Copy)
+        w2_words = keep.tile([P, N], U32, name="w2_words", align_bytes=64)
+        w2_scales = keep.tile([P, N], U8, name="w2_scales", align_bytes=64)
         nc.vector.quantize_mx(
             out=w2_words[:].bitcast(FP8X4), scales=w2_scales[:], in_=w2_bf[:].rearrange("p c j -> p (c j)")
         )
-        hop1_gathers(1)
-        second_product(0, z_first)
-        second_product(1, hop1_sum(1))
+        gate_last = keep.tile([P, 2, V - split], F32, name="gate_last", tag="gate0")
+        nc.scalar.copy(gate_last[:], gate_rest[:])
+        gates[1, 0] = gate_last[:, 0, :]
+        gates[1, 1] = gate_last[:, 1, :]
+        second_product(0)
+        hop1(1)
+        second_product(1)
 
         for b in range(N // P):
             pair = keep.tile([P, 2, U], F32, name=f"pair{b}")

@@ -22,15 +22,20 @@ PACK = 4
 K_PASS = P * PACK
 PASSES = K // K_PASS
 BANK = 512
+H_TILES = H // P
+G_TILES = N // P
 X_CHUNKS = [[512, 512, 512, 512], [512, 512, 512, 256, 256]]
 SCALAR_NODES = {512: 256, 256: 96}
 W1_CHUNK = 256
-V_SLICES = [(0, 384), (384, 512)]
-Z_SPANS = [[(0, 256), (256, 384)], [(384, 512)]]
+V_SPLIT = 384
 
 
 def interleave_views(dst, src):
     return (dst.rearrange("p (c i) j -> p c j i", i=4), src.rearrange("p j (c i) -> p c j i", i=4))
+
+
+def entries(offsets, e0, e1):
+    return offsets[:, e0 // 16 : e1 // 16]
 
 
 def tile_picked_hop2_gelu_e_kernel(tc, xT, w1, w2, gate, gate2, offs, pos1, pos2, nxt1, nxt2, out):
@@ -44,6 +49,14 @@ def tile_picked_hop2_gelu_e_kernel(tc, xT, w1, w2, gate, gate2, offs, pos1, pos2
             nc.sync.dma_start(tile[:], src)
             return tile
 
+        def load_rows(name, rows):
+            tile = keep.tile([P, PACK, rows.shape[1]], F32, name=name, tag=name, align_bytes=64)
+            nc.sync.dma_start(tile[:], rows.rearrange("(p j) c -> p j c", j=PACK))
+            return tile
+
+        def quantize(words, scales, values):
+            nc.vector.quantize_mx(out=words.bitcast(FP8X4), scales=scales, in_=values)
+
         warm = keep.tile([P, 2], F32, name="warm")
         nc.vector.memset(warm[:, 0:1], 0.0)
         nc.scalar.activation(warm[:, 1:2], warm[:, 0:1], ACT.Gelu_apprx_tanh)
@@ -55,58 +68,39 @@ def tile_picked_hop2_gelu_e_kernel(tc, xT, w1, w2, gate, gate2, offs, pos1, pos2
         x_words = [keep.tile([P, T], U32, name=f"x_words{g}", tag=f"x_words{g}", align_bytes=64) for g in range(PASSES)]
 
         x_raw = {}
-        lists = {}
         for g in range(PASSES):
             c0 = 0
             for width in X_CHUNKS[g]:
-                raw = keep.tile([P, PACK, width], F32, name=f"x_raw{g}_{c0}")
-                rows = xT[g * K_PASS : (g + 1) * K_PASS, c0 : c0 + width]
-                nc.sync.dma_start(raw[:], rows.rearrange("(p j) c -> p j c", j=PACK))
-                x_raw[g, c0] = raw
+                x_raw[g, c0] = load_rows(f"x_raw{g}_{c0}", xT[g * K_PASS : (g + 1) * K_PASS, c0 : c0 + width])
                 c0 = c0 + width
-                if g == 0 and c0 == 1024:
-                    lists["offs"] = load_list("offs", offs)
-                    lists["pos1"] = load_list("pos1", pos1)
-                    lists["pos2"] = load_list("pos2", pos2)
+            if g == 0:
+                offs_sb = load_list("offs_sb", offs)
         w1_raw = {}
         for c0 in range(0, H, W1_CHUNK):
             for g in range(PASSES):
-                raw = keep.tile([P, PACK, W1_CHUNK], F32, name=f"w1_raw{g}_{c0}")
-                rows = w1[g * K_PASS : (g + 1) * K_PASS, c0 : c0 + W1_CHUNK]
-                nc.sync.dma_start(raw[:], rows.rearrange("(p j) c -> p j c", j=PACK))
-                w1_raw[g, c0] = raw
-        split = V_SLICES[0][1]
-        gates = {}
-        for d in range(2):
-            gates[0, d] = keep.tile([P, split], F32, name=f"gate_first{d}", tag=f"gate{d}")[:]
-            nc.sync.dma_start(gates[0, d], gate[d, :, :split])
-        gate_rest = keep.tile([P, 2, V - split], F32, name="gate_rest")
-        nc.sync.dma_start(gate_rest[:], gate[:, :, split:].rearrange("d p v -> p d v"))
-        w2_raw = keep.tile([P, PACK, N], F32, name="w2_raw")
-        nc.sync.dma_start(w2_raw[:], w2.rearrange("(p j) c -> p j c", j=PACK))
+                w1_raw[g, c0] = load_rows(f"w1_raw{g}_{c0}", w1[g * K_PASS : (g + 1) * K_PASS, c0 : c0 + W1_CHUNK])
+        pos_sb = [load_list("pos1_sb", pos1), load_list("pos2_sb", pos2)]
+        gate_sb = keep.tile([P, 2, V], F32, name="gate_sb")
+        nc.sync.dma_start(gate_sb[:], gate.rearrange("d p v -> p d v"))
+        w2_raw = load_rows("w2_raw", w2)
         gate2_sb = keep.tile([P, 2, U], F32, name="gate2_sb")
         nc.sync.dma_start(gate2_sb[:], gate2.rearrange("d p v -> p d v"))
-        lists["nxt1"] = load_list("nxt1", nxt1)
-        lists["nxt2"] = load_list("nxt2", nxt2)
+        nxt_sb = [load_list("nxt1_sb", nxt1), load_list("nxt2_sb", nxt2)]
 
-        halves = range(S // BANK)
         picked_words = {}
         picked_scales = {}
-
-        def offs_half(half):
-            return lists["offs"][:, half * BANK // 16 : (half + 1) * BANK // 16]
 
         def gather_words(g, half, tag, pieces=1):
             tile = keep.tile([P, BANK], U32, name=f"picked_words{g}_{half}", tag=tag, align_bytes=64)
             step = BANK // pieces
             for e0 in range(0, BANK, step):
-                entries = offs_half(half)[:, e0 // 16 : (e0 + step) // 16]
-                nc.vector.tensor_copy(tile[:, e0 : e0 + step], x_words[g][:].indirect(entries))
+                piece = entries(offs_sb, half * BANK + e0, half * BANK + e0 + step)
+                nc.vector.tensor_copy(tile[:, e0 : e0 + step], x_words[g][:].indirect(piece))
             picked_words[g, half] = tile
 
         def gather_scales(half, tag):
             tile = keep.tile([P, BANK], U8, name=f"picked_scales{half}", tag=tag, align_bytes=64)
-            nc.vector.tensor_copy(tile[:], x_scales[:].indirect(offs_half(half)))
+            nc.vector.tensor_copy(tile[:], x_scales[:].indirect(entries(offs_sb, half * BANK, (half + 1) * BANK)))
             picked_scales[half] = tile
 
         for g in range(PASSES):
@@ -121,51 +115,52 @@ def tile_picked_hop2_gelu_e_kernel(tc, xT, w1, w2, gate, gate2, offs, pos1, pos2
                 nc.vector.tensor_copy(dst, src)
                 if g == 1 and n < 2:
                     gather_words(0, n, f"words0_{n}")
-                nc.vector.quantize_mx(
-                    out=x_words[g][:, c0 : c0 + width].bitcast(FP8X4),
-                    scales=x_scales[4 * g :, c0 : c0 + width],
-                    in_=grouped[:].rearrange("p c j -> p (c j)"),
+                quantize(
+                    x_words[g][:, c0 : c0 + width],
+                    x_scales[4 * g :, c0 : c0 + width],
+                    grouped[:].rearrange("p c j -> p (c j)"),
                 )
                 c0 = c0 + width
 
-        w1_words, w1_scales = {}, {}
-
-        def quantize_w1(g, c, words):
+        w1_bf = []
+        for c in range(H_TILES):
             c0, m0 = c * P // W1_CHUNK * W1_CHUNK, c * P % W1_CHUNK
-            grouped = keep.tile([P, P, PACK], BF16, name=f"w1_bf{g}_{c}", tag=f"w1_bf{g}_{c}", align_bytes=64)
-            dst, src = interleave_views(grouped[:], w1_raw[g, c0][:, :, m0 : m0 + P])
-            nc.scalar.activation(dst, src, ACT.Copy)
-            w1_words[g, c] = words
-            w1_scales[g, c] = keep.tile([P, P], U8, name=f"w1_scales{g}_{c}", align_bytes=64)
-            nc.vector.quantize_mx(
-                out=words.bitcast(FP8X4), scales=w1_scales[g, c][:], in_=grouped[:].rearrange("p c j -> p (c j)")
-            )
+            grouped = keep.tile([P, PASSES, P, PACK], BF16, name=f"w1_bf{c}", tag=f"w1_bf{c}", align_bytes=64)
+            for g in range(PASSES):
+                dst, src = interleave_views(grouped[:, g], w1_raw[g, c0][:, :, m0 : m0 + P])
+                nc.scalar.activation(dst, src, ACT.Copy)
+            w1_bf.append(grouped)
+        w1_words, w1_scales = [], []
 
-        first_words = keep.tile([P, PASSES, P], U32, name="w1_first", align_bytes=64)
+        def quantize_w1(c, words):
+            scales = keep.tile([P, PASSES * P], U8, name=f"w1_scales{c}", align_bytes=64)
+            quantize(words, scales[:], w1_bf[c][:].rearrange("p g c j -> p (g c j)"))
+            w1_words.append(words)
+            w1_scales.append(scales)
+
+        first_words = keep.tile([P, PASSES * P], U32, name="w1_first", align_bytes=64)
         gather_scales(0, "scales0")
         gather_words(1, 0, "words1_0")
-        quantize_w1(0, 0, first_words[:, 0, :])
-        quantize_w1(1, 0, first_words[:, 1, :])
-        gather_scales(1, "w1_bf0_0")
-        gather_words(1, 1, "w1_bf1_0", 2)
-        later_words = keep.tile([P, PASSES, H - P], U32, name="w1_later", tag="x_words1", align_bytes=64)
-        for c in range(1, H // P):
-            for g in range(PASSES):
-                quantize_w1(g, c, later_words[:, g, (c - 1) * P : c * P])
+        quantize_w1(0, first_words[:])
+        gather_scales(1, "w1_bf0")
+        gather_words(1, 1, "w1_raw1_0", 2)
+        later_words = keep.tile([P, H_TILES - 1, PASSES * P], U32, name="w1_later", tag="x_words1", align_bytes=64)
+        for c in range(1, H_TILES):
+            quantize_w1(c, later_words[:, c - 1, :])
 
         h = []
         groups = 0
-        for c in range(H // P):
+        for c in range(H_TILES):
             spans = [(0, 0, BANK), (1, 0, BANK // 2), (1, BANK // 2, BANK)] if c == 0 else [(0, 0, BANK), (1, 0, BANK)]
-            h_c = keep.tile([P, S], F32, name=f"h{c}")
+            h_c = keep.tile([P, S], F32, name=f"h{c}", tag=f"h{c}", align_bytes=64)
             for half, e0, e1 in spans:
                 acc = psum.tile([P, BANK], F32, name=f"acc{groups}", tag=f"bank{groups % 4}")
                 groups = groups + 1
                 for g in range(PASSES):
                     nc.tensor.matmul_mx(
                         out=acc[:, : e1 - e0],
-                        lhsT=w1_words[g, c].bitcast(FP8X4),
-                        lhsT_scale=w1_scales[g, c][:],
+                        lhsT=w1_words[c][:, g * P : (g + 1) * P].bitcast(FP8X4),
+                        lhsT_scale=w1_scales[c][:, g * P : (g + 1) * P],
                         rhs=picked_words[g, half][:, e0:e1].bitcast(FP8X4),
                         rhs_scale=picked_scales[half][4 * g :, e0:e1],
                         start=(g == 0),
@@ -176,23 +171,17 @@ def tile_picked_hop2_gelu_e_kernel(tc, xT, w1, w2, gate, gate2, offs, pos1, pos2
                 )
             h.append(h_c)
 
-        g_sb = [keep.tile([P, V], F32, name=f"g{b}") for b in range(N // P)]
-        z_rows = {}
-
-        def hop1(s):
-            v0, v1 = V_SLICES[s]
+        def hop1(s, v0, v1):
             blocks = (v1 - v0) // P
-            z_rows[s] = keep.tile([P, blocks, 2, P, 2], BF16, name=f"z_rows{s}")
-            for c in range(H // P):
-                terms = keep.tile([P, 2, v1 - v0], F32, name=f"terms{s}_{c}")
-                for d, name in enumerate(("pos1", "pos2")):
+            z_rows = keep.tile([P, blocks, 2, P, 2], BF16, name=f"z_rows{s}")
+            for n in range(H_TILES):
+                c = (n - s) % H_TILES
+                terms = keep.tile([P, 2, v1 - v0], F32, name=f"terms{s}_{c}", tag=f"terms{n}")
+                for d in range(2):
                     nc.vector.tensor_tensor(
-                        terms[:, d, :],
-                        h[c][:].indirect(lists[name][:, v0 // 16 : v1 // 16]),
-                        gates[s, d],
-                        MULT,
+                        terms[:, d, :], h[c][:].indirect(entries(pos_sb[d], v0, v1)), gate_sb[:, d, v0:v1], MULT
                     )
-                turned = psum.tile([P, blocks, P], F32, name=f"turned{s}_{c}", tag=f"bank{4 + c % 2}")
+                turned = psum.tile([P, blocks, P], F32, name=f"turned{s}_{c}", tag=f"bank{4 + n % 2}")
                 for vb in range(blocks):
                     for d in range(2):
                         nc.tensor.matmul(
@@ -204,67 +193,70 @@ def tile_picked_hop2_gelu_e_kernel(tc, xT, w1, w2, gate, gate2, offs, pos1, pos2
                             is_transpose=True,
                         )
                 nc.scalar.copy(
-                    z_rows[s][:, :, :, 32 * c : 32 * (c + 1), :],
+                    z_rows[:, :, :, 32 * c : 32 * (c + 1), :],
                     turned[:].rearrange("v b (q u e) -> v b u q e", u=2, e=2),
                 )
+            return z_rows
 
-        banks = [0]
+        def turn_back(z_rows, b0, b1, z_bf, bank, engine_copy):
+            row_words = z_rows[:].rearrange("v b u p e -> v (b u p e)").bitcast(F32)
+            back = psum.tile([P, b1 - b0, 2, P], F32, name=f"back{bank}", tag=f"bank{bank}")
+            for vb in range(b0, b1):
+                for u in range(2):
+                    w0 = (vb * 2 + u) * P
+                    nc.tensor.transpose(back[:, vb - b0, u, :], row_words[:, w0 : w0 + P], ident[:])
+            engine_copy(
+                z_bf[:, b0 * K_PASS : b1 * K_PASS].bitcast(F32).rearrange("p (b v u) -> p b v u", u=2, v=P),
+                back[:].rearrange("p b u v -> p b v u"),
+            )
 
-        def second_product(s):
-            base = V_SLICES[s][0]
-            row_words = z_rows[s][:].rearrange("v b u p e -> v (b u p e)").bitcast(F32)
-            for v0, v1 in Z_SPANS[s]:
-                blocks = (v1 - v0) // P
-                back = psum.tile([P, blocks, 2, P], F32, name=f"back{v0}", tag=f"bank{6 + banks[0] // 2 % 2}")
-                for vb in range(blocks):
-                    for u in range(2):
-                        w0 = (((v0 - base) // P + vb) * 2 + u) * P
-                        nc.tensor.transpose(back[:, vb, u, :], row_words[:, w0 : w0 + P], ident[:])
-                z_bf = keep.tile([P, (v1 - v0) * PACK], BF16, name=f"z_bf{v0}", align_bytes=64)
-                dst = z_bf[:].bitcast(F32).rearrange("p (b v u) -> p b v u", u=2, v=P)
-                src = back[:].rearrange("p b u v -> p b v u")
-                if s == len(V_SLICES) - 1:
-                    nc.vector.tensor_copy(dst, src)
-                else:
-                    nc.scalar.copy(dst, src)
-                words = keep.tile([P, v1 - v0], U32, name=f"z_words{v0}", align_bytes=64)
-                scales = keep.tile([P, v1 - v0], U8, name=f"z_scales{v0}", align_bytes=64)
-                nc.vector.quantize_mx(out=words[:].bitcast(FP8X4), scales=scales[:], in_=z_bf[:])
-                for b in range(N // P):
-                    bank = psum.tile([P, BANK], F32, name=f"g_acc{v0}_{b}", tag=f"bank{banks[0] % 4}")
-                    banks[0] = banks[0] + 1
-                    nc.tensor.matmul_mx(
-                        out=bank[:, : v1 - v0],
-                        lhsT=w2_words[:, b * P : (b + 1) * P].bitcast(FP8X4),
-                        lhsT_scale=w2_scales[:, b * P : (b + 1) * P],
-                        rhs=words[:].bitcast(FP8X4),
-                        rhs_scale=scales[:],
-                        start=True,
-                        stop=True,
-                    )
-                    nc.scalar.activation(g_sb[b][:, v0:v1], bank[:, : v1 - v0], ACT.Relu)
-
-        hop1(0)
+        z_bf = [
+            keep.tile([P, V_SPLIT * PACK], BF16, name="z_bf0", align_bytes=64),
+            keep.tile([P, (V - V_SPLIT) * PACK], BF16, name="z_bf1", align_bytes=64),
+        ]
+        z_rows = hop1(0, 0, V_SPLIT)
         w2_bf = keep.tile([P, N, PACK], BF16, name="w2_bf", tag="words0_1", align_bytes=64)
         dst, src = interleave_views(w2_bf[:], w2_raw[:])
         nc.scalar.activation(dst, src, ACT.Copy)
-        w2_words = keep.tile([P, N], U32, name="w2_words", align_bytes=64)
-        w2_scales = keep.tile([P, N], U8, name="w2_scales", align_bytes=64)
-        nc.vector.quantize_mx(
-            out=w2_words[:].bitcast(FP8X4), scales=w2_scales[:], in_=w2_bf[:].rearrange("p c j -> p (c j)")
-        )
-        gate_last = keep.tile([P, 2, V - split], F32, name="gate_last", tag="gate0")
-        nc.scalar.copy(gate_last[:], gate_rest[:])
-        gates[1, 0] = gate_last[:, 0, :]
-        gates[1, 1] = gate_last[:, 1, :]
-        second_product(0)
-        hop1(1)
-        second_product(1)
+        turn_back(z_rows, 0, 2, z_bf[0], 6, nc.scalar.copy)
+        turn_back(z_rows, 2, 3, z_bf[0], 7, nc.scalar.copy)
+        z_rows = hop1(1, V_SPLIT, V)
 
-        for b in range(N // P):
+        late_words = keep.tile([P, N + V], U32, name="late_words", tag="h2", align_bytes=64)
+        late_scales = keep.tile([P, N + V], U8, name="late_scales", align_bytes=64)
+        quantize(late_words[:, :N], late_scales[:, :N], w2_bf[:].rearrange("p c j -> p (c j)"))
+        g_sb = [keep.tile([P, V], F32, name=f"g{b}") for b in range(G_TILES)]
+
+        def second_product(s, spans):
+            base, end = spans[0][0], spans[-1][1]
+            banks = [psum.tile([P, BANK], F32, name=f"g_acc{s}_{b}", tag=f"bank{2 * s + b}") for b in range(G_TILES)]
+            for v0, v1 in spans:
+                words, scales = late_words[:, N + v0 : N + v1], late_scales[:, N + v0 : N + v1]
+                quantize(words, scales, z_bf[s][:, (v0 - base) * PACK : (v1 - base) * PACK])
+                for b in range(G_TILES):
+                    nc.tensor.matmul_mx(
+                        out=banks[b][:, v0 - base : v1 - base],
+                        lhsT=late_words[:, b * P : (b + 1) * P].bitcast(FP8X4),
+                        lhsT_scale=late_scales[:, b * P : (b + 1) * P],
+                        rhs=words.bitcast(FP8X4),
+                        rhs_scale=scales,
+                        start=True,
+                        stop=True,
+                    )
+            for b in range(G_TILES):
+                if s == 0 and b == 1:
+                    nc.vector.tensor_scalar_max(g_sb[b][:, base:end], banks[b][:, : end - base], 0.0)
+                else:
+                    nc.scalar.activation(g_sb[b][:, base:end], banks[b][:, : end - base], ACT.Relu)
+
+        second_product(0, [(0, 256), (256, V_SPLIT)])
+        turn_back(z_rows, 0, 1, z_bf[1], 6, nc.vector.tensor_copy)
+        second_product(1, [(V_SPLIT, V)])
+
+        for b in range(G_TILES):
             pair = keep.tile([P, 2, U], F32, name=f"pair{b}")
-            for d, name in enumerate(("nxt1", "nxt2")):
-                nc.vector.tensor_tensor(pair[:, d, :], g_sb[b][:].indirect(lists[name][:]), gate2_sb[:, d, :], MULT)
+            for d in range(2):
+                nc.vector.tensor_tensor(pair[:, d, :], g_sb[b][:].indirect(nxt_sb[d][:]), gate2_sb[:, d, :], MULT)
             result = keep.tile([P, U], F32, name=f"result{b}")
             nc.vector.tensor_tensor(result[:], pair[:, 0, :], pair[:, 1, :], ADD)
             nc.sync.dma_start(out[b * P : (b + 1) * P, :], result[:])

@@ -1,7 +1,6 @@
 from contextlib import ExitStack
 
 import concourse.mybir as mybir
-from concourse.masks import make_identity
 
 K, T, S, V, H, N, U = 1024, 2048, 1024, 512, 512, 256, 256
 FLOPS = 2 * K * H * S + 2 * H * N * V
@@ -9,7 +8,6 @@ FLOPS = 2 * K * H * S + 2 * H * N * V
 F32 = mybir.dt.float32
 BF16 = mybir.dt.bfloat16
 U32 = mybir.dt.uint32
-I32 = mybir.dt.int32
 U16 = mybir.dt.uint16
 U8 = mybir.dt.uint8
 FP8X4 = mybir.dt.float8_e4m3fn_x4
@@ -22,12 +20,11 @@ PACK = 4
 K_PASS = P * PACK
 PASSES = K // K_PASS
 BANK = 512
-H_TILES = H // P
+HALVES = S // BANK
 G_TILES = N // P
-X_CHUNKS = [[512, 512, 512, 512], [512, 512, 512, 256, 256]]
-SCALAR_NODES = {512: 256, 256: 96}
-W1_CHUNK = 256
-V_SPLIT = 384
+VECTOR_ENTRIES = 384
+VECTOR_ENTRIES_LAST = 256
+V_SLICES = [(0, 256), (256, 512)]
 
 
 def interleave_views(dst, src):
@@ -49,9 +46,14 @@ def tile_picked_hop2_gelu_e_kernel(tc, xT, w1, w2, gate, gate2, offs, pos1, pos2
             nc.sync.dma_start(tile[:], src)
             return tile
 
-        def load_rows(name, rows):
-            tile = keep.tile([P, PACK, rows.shape[1]], F32, name=name, tag=name, align_bytes=64)
-            nc.sync.dma_start(tile[:], rows.rearrange("(p j) c -> p j c", j=PACK))
+        def load_plane(g, j):
+            tile = keep.tile([P, T], F32, name=f"x_plane{g}_{j}")
+            nc.sync.dma_start(tile[:], xT[g * K_PASS : (g + 1) * K_PASS, :].rearrange("(p j) c -> j p c", j=PACK)[j])
+            return tile
+
+        def load_w1(g):
+            tile = keep.tile([P, PACK, H], F32, name=f"w1_raw{g}")
+            nc.sync.dma_start(tile[:], w1[g * K_PASS : (g + 1) * K_PASS, :].rearrange("(p j) c -> p j c", j=PACK))
             return tile
 
         def quantize(words, scales, values):
@@ -60,203 +62,205 @@ def tile_picked_hop2_gelu_e_kernel(tc, xT, w1, w2, gate, gate2, offs, pos1, pos2
         warm = keep.tile([P, 2], F32, name="warm")
         nc.vector.memset(warm[:, 0:1], 0.0)
         nc.scalar.activation(warm[:, 1:2], warm[:, 0:1], ACT.Gelu_apprx_tanh)
-        ident = keep.tile([P, P], F32, name="ident")
-        make_identity(nc, ident[:])
 
-        x_scales = keep.tile([P, T], U8, name="x_scales", align_bytes=64)
-        nc.vector.memset(x_scales[:].bitcast(I32), 0)
-        x_words = [keep.tile([P, T], U32, name=f"x_words{g}", tag=f"x_words{g}", align_bytes=64) for g in range(PASSES)]
-
-        x_raw = {}
-        for g in range(PASSES):
-            c0 = 0
-            for width in X_CHUNKS[g]:
-                x_raw[g, c0] = load_rows(f"x_raw{g}_{c0}", xT[g * K_PASS : (g + 1) * K_PASS, c0 : c0 + width])
-                c0 = c0 + width
-            if g == 0:
-                offs_sb = load_list("offs_sb", offs)
-        w1_raw = {}
-        for c0 in range(0, H, W1_CHUNK):
-            for g in range(PASSES):
-                w1_raw[g, c0] = load_rows(f"w1_raw{g}_{c0}", w1[g * K_PASS : (g + 1) * K_PASS, c0 : c0 + W1_CHUNK])
+        planes = {(0, 0): load_plane(0, 0)}
+        offs_sb = load_list("offs_sb", offs)
+        for n in range(1, PASSES * PACK - 1):
+            planes[n // PACK, n % PACK] = load_plane(n // PACK, n % PACK)
+        w1_raw = [load_w1(0)]
+        planes[1, 3] = load_plane(1, 3)
+        w1_raw.append(load_w1(1))
         pos_sb = [load_list("pos1_sb", pos1), load_list("pos2_sb", pos2)]
         gate_sb = keep.tile([P, 2, V], F32, name="gate_sb")
         nc.sync.dma_start(gate_sb[:], gate.rearrange("d p v -> p d v"))
-        w2_raw = load_rows("w2_raw", w2)
+        w2_raw = keep.tile([P, PACK, N], F32, name="w2_raw")
+        for t in range(PACK):
+            nc.sync.dma_start(w2_raw[:, t, :], w2.rearrange("(a t r) n -> t a r n", t=PACK, r=4)[t])
         gate2_sb = keep.tile([P, 2, U], F32, name="gate2_sb")
         nc.sync.dma_start(gate2_sb[:], gate2.rearrange("d p v -> p d v"))
         nxt_sb = [load_list("nxt1_sb", nxt1), load_list("nxt2_sb", nxt2)]
 
-        picked_words = {}
-        picked_scales = {}
-
-        def gather_words(g, half, tag, pieces=1):
-            tile = keep.tile([P, BANK], U32, name=f"picked_words{g}_{half}", tag=tag, align_bytes=64)
-            step = BANK // pieces
-            for e0 in range(0, BANK, step):
-                piece = entries(offs_sb, half * BANK + e0, half * BANK + e0 + step)
-                nc.vector.tensor_copy(tile[:, e0 : e0 + step], x_words[g][:].indirect(piece))
-            picked_words[g, half] = tile
-
-        def gather_scales(half, tag):
-            tile = keep.tile([P, BANK], U8, name=f"picked_scales{half}", tag=tag, align_bytes=64)
-            nc.vector.tensor_copy(tile[:], x_scales[:].indirect(entries(offs_sb, half * BANK, (half + 1) * BANK)))
-            picked_scales[half] = tile
-
+        picked = {}
+        x_bf = {}
+        x_words = {}
+        x_scales = {}
         for g in range(PASSES):
-            c0 = 0
-            for n, width in enumerate(X_CHUNKS[g]):
-                raw = x_raw[g, c0]
-                grouped = keep.tile([P, width, PACK], BF16, name=f"x_bf{g}_{c0}", align_bytes=64)
-                cut = SCALAR_NODES[width]
-                dst, src = interleave_views(grouped[:, :cut, :], raw[:, :, :cut])
-                nc.scalar.activation(dst, src, ACT.Copy)
-                dst, src = interleave_views(grouped[:, cut:, :], raw[:, :, cut:])
-                nc.vector.tensor_copy(dst, src)
-                if g == 1 and n < 2:
-                    gather_words(0, n, f"words0_{n}")
-                quantize(
-                    x_words[g][:, c0 : c0 + width],
-                    x_scales[4 * g :, c0 : c0 + width],
-                    grouped[:].rearrange("p c j -> p (c j)"),
-                )
-                c0 = c0 + width
+            for u in range(HALVES):
+                picked[g, u] = keep.tile([P, PACK, BANK], F32, name=f"picked{g}_{u}")
+                x_bf[g, u] = keep.tile([P, BANK, PACK], BF16, name=f"x_bf{g}_{u}", align_bytes=64)
+                x_words[g, u] = keep.tile([P, BANK], U32, name=f"x_words{g}_{u}", align_bytes=64)
+                x_scales[g, u] = keep.tile([P, BANK], U8, name=f"x_scales{g}_{u}", align_bytes=64)
 
-        w1_bf = []
-        for c in range(H_TILES):
-            c0, m0 = c * P // W1_CHUNK * W1_CHUNK, c * P % W1_CHUNK
-            grouped = keep.tile([P, PASSES, P, PACK], BF16, name=f"w1_bf{c}", tag=f"w1_bf{c}", align_bytes=64)
-            for g in range(PASSES):
-                dst, src = interleave_views(grouped[:, g], w1_raw[g, c0][:, :, m0 : m0 + P])
-                nc.scalar.activation(dst, src, ACT.Copy)
-            w1_bf.append(grouped)
-        w1_words, w1_scales = [], []
+        def gather_plane(g, j, cut):
+            window = planes[g, j][:]
+            nc.vector.tensor_copy(picked[g, 0][:, j, :cut], window.indirect(entries(offs_sb, 0, cut)))
+            nc.scalar.activation(picked[g, 0][:, j, cut:], window.indirect(entries(offs_sb, cut, BANK)), ACT.Copy)
+            nc.scalar.activation(picked[g, 1][:, j, :], window.indirect(entries(offs_sb, BANK, S)), ACT.Copy)
 
-        def quantize_w1(c, words):
-            scales = keep.tile([P, PASSES * P], U8, name=f"w1_scales{c}", align_bytes=64)
-            quantize(words, scales[:], w1_bf[c][:].rearrange("p g c j -> p (g c j)"))
-            w1_words.append(words)
-            w1_scales.append(scales)
+        def interleave_x(g, u):
+            dst, src = interleave_views(x_bf[g, u][:], picked[g, u][:])
+            nc.vector.tensor_copy(dst, src)
 
-        first_words = keep.tile([P, PASSES * P], U32, name="w1_first", align_bytes=64)
-        gather_scales(0, "scales0")
-        gather_words(1, 0, "words1_0")
-        quantize_w1(0, first_words[:])
-        gather_scales(1, "w1_bf0")
-        gather_words(1, 1, "w1_raw1_0", 2)
-        later_words = keep.tile([P, H_TILES - 1, PASSES * P], U32, name="w1_later", tag="x_words1", align_bytes=64)
-        for c in range(1, H_TILES):
-            quantize_w1(c, later_words[:, c - 1, :])
+        def quantize_x(g, u):
+            quantize(x_words[g, u][:], x_scales[g, u][:], x_bf[g, u][:].rearrange("p c j -> p (c j)"))
 
-        h = []
-        groups = 0
-        for c in range(H_TILES):
-            spans = [(0, 0, BANK), (1, 0, BANK // 2), (1, BANK // 2, BANK)] if c == 0 else [(0, 0, BANK), (1, 0, BANK)]
-            h_c = keep.tile([P, S], F32, name=f"h{c}", tag=f"h{c}", align_bytes=64)
-            for half, e0, e1 in spans:
-                acc = psum.tile([P, BANK], F32, name=f"acc{groups}", tag=f"bank{groups % 4}")
-                groups = groups + 1
-                for g in range(PASSES):
-                    nc.tensor.matmul_mx(
-                        out=acc[:, : e1 - e0],
-                        lhsT=w1_words[c][:, g * P : (g + 1) * P].bitcast(FP8X4),
-                        lhsT_scale=w1_scales[c][:, g * P : (g + 1) * P],
-                        rhs=picked_words[g, half][:, e0:e1].bitcast(FP8X4),
-                        rhs_scale=picked_scales[half][4 * g :, e0:e1],
-                        start=(g == 0),
-                        stop=(g == PASSES - 1),
-                    )
-                nc.scalar.activation(
-                    h_c[:, half * BANK + e0 : half * BANK + e1], acc[:, : e1 - e0], ACT.Gelu_apprx_tanh
-                )
-            h.append(h_c)
+        w1_bf, w1_words, w1_scales = {}, {}, {}
 
-        def hop1(s, v0, v1):
-            blocks = (v1 - v0) // P
-            z_rows = keep.tile([P, blocks, 2, P, 2], BF16, name=f"z_rows{s}")
-            for n in range(H_TILES):
-                c = (n - s) % H_TILES
-                terms = keep.tile([P, 2, v1 - v0], F32, name=f"terms{s}_{c}", tag=f"terms{n}")
-                for d in range(2):
-                    nc.vector.tensor_tensor(
-                        terms[:, d, :], h[c][:].indirect(entries(pos_sb[d], v0, v1)), gate_sb[:, d, v0:v1], MULT
-                    )
-                turned = psum.tile([P, blocks, P], F32, name=f"turned{s}_{c}", tag=f"bank{4 + n % 2}")
-                for vb in range(blocks):
-                    for d in range(2):
-                        nc.tensor.matmul(
-                            turned[:, vb, :],
-                            terms[:, d, vb * P : (vb + 1) * P],
-                            ident[:],
-                            start=(d == 0),
-                            stop=(d == 1),
-                            is_transpose=True,
-                        )
-                nc.scalar.copy(
-                    z_rows[:, :, :, 32 * c : 32 * (c + 1), :],
-                    turned[:].rearrange("v b (q u e) -> v b u q e", u=2, e=2),
-                )
-            return z_rows
+        def round_w1(g, t0, t1, copy):
+            grouped = keep.tile([P, t1 - t0, P, PACK], BF16, name=f"w1_bf{g}_{t0}", align_bytes=64)
+            copy(
+                grouped[:].rearrange("p t (a r) j -> p t a j r", r=4),
+                w1_raw[g][:].rearrange("p j (a t r) -> p t a j r", t=PACK, r=4)[:, t0:t1],
+            )
+            w1_bf[g, t0] = grouped
 
-        def turn_back(z_rows, b0, b1, z_bf, bank, engine_copy):
-            row_words = z_rows[:].rearrange("v b u p e -> v (b u p e)").bitcast(F32)
-            back = psum.tile([P, b1 - b0, 2, P], F32, name=f"back{bank}", tag=f"bank{bank}")
-            for vb in range(b0, b1):
-                for u in range(2):
-                    w0 = (vb * 2 + u) * P
-                    nc.tensor.transpose(back[:, vb - b0, u, :], row_words[:, w0 : w0 + P], ident[:])
-            engine_copy(
-                z_bf[:, b0 * K_PASS : b1 * K_PASS].bitcast(F32).rearrange("p (b v u) -> p b v u", u=2, v=P),
-                back[:].rearrange("p b u v -> p b v u"),
+        def quantize_w1(g, t0, t1):
+            words = keep.tile([P, (t1 - t0) * P], U32, name=f"w1_words{g}_{t0}", align_bytes=64)
+            scales = keep.tile([P, (t1 - t0) * P], U8, name=f"w1_scales{g}_{t0}", align_bytes=64)
+            quantize(words[:], scales[:], w1_bf[g, t0][:].rearrange("p t m j -> p (t m j)"))
+            for t in range(t0, t1):
+                w1_words[g, t] = words[:, (t - t0) * P : (t - t0 + 1) * P]
+                w1_scales[g, t] = scales[:, (t - t0) * P : (t - t0 + 1) * P]
+
+        acc = {}
+
+        def first_product(g, t, u):
+            if g == 0:
+                acc[t, u] = psum.tile([P, BANK], F32, name=f"acc{t}_{u}", tag=f"bank{2 * t + u}")
+            nc.tensor.matmul_mx(
+                out=acc[t, u][:],
+                lhsT=w1_words[g, t].bitcast(FP8X4),
+                lhsT_scale=w1_scales[g, t],
+                rhs=x_words[g, u][:].bitcast(FP8X4),
+                rhs_scale=x_scales[g, u][:],
+                start=(g == 0),
+                stop=(g == PASSES - 1),
             )
 
-        z_bf = [
-            keep.tile([P, V_SPLIT * PACK], BF16, name="z_bf0", align_bytes=64),
-            keep.tile([P, (V - V_SPLIT) * PACK], BF16, name="z_bf1", align_bytes=64),
-        ]
-        z_rows = hop1(0, 0, V_SPLIT)
-        w2_bf = keep.tile([P, N, PACK], BF16, name="w2_bf", tag="words0_1", align_bytes=64)
-        dst, src = interleave_views(w2_bf[:], w2_raw[:])
-        nc.scalar.activation(dst, src, ACT.Copy)
-        turn_back(z_rows, 0, 2, z_bf[0], 6, nc.scalar.copy)
-        turn_back(z_rows, 2, 3, z_bf[0], 7, nc.scalar.copy)
-        z_rows = hop1(1, V_SPLIT, V)
+        for j in range(PACK):
+            gather_plane(0, j, VECTOR_ENTRIES)
+        interleave_x(0, 0)
+        gather_plane(1, 0, VECTOR_ENTRIES)
+        quantize_x(0, 0)
+        interleave_x(0, 1)
+        gather_plane(1, 1, VECTOR_ENTRIES)
+        quantize_x(0, 1)
+        gather_plane(1, 2, VECTOR_ENTRIES)
+        round_w1(0, 0, 2, nc.vector.tensor_copy)
+        round_w1(0, 2, 4, nc.scalar.copy)
+        quantize_w1(0, 0, 2)
+        quantize_w1(0, 2, 4)
+        for t in range(PACK):
+            for u in range(HALVES):
+                first_product(0, t, u)
+        gather_plane(1, 3, VECTOR_ENTRIES_LAST)
+        interleave_x(1, 0)
+        interleave_x(1, 1)
+        quantize_x(1, 0)
+        for t in range(PACK):
+            round_w1(1, t, t + 1, nc.scalar.copy)
+        quantize_w1(1, 0, 1)
+        quantize_x(1, 1)
+        for t in range(1, PACK):
+            quantize_w1(1, t, t + 1)
 
-        late_words = keep.tile([P, N + V], U32, name="late_words", tag="h2", align_bytes=64)
-        late_scales = keep.tile([P, N + V], U8, name="late_scales", align_bytes=64)
-        quantize(late_words[:, :N], late_scales[:, :N], w2_bf[:].rearrange("p c j -> p (c j)"))
+        h = [keep.tile([P, S], F32, name=f"h{t}") for t in range(PACK)]
+        for t in range(PACK):
+            for u in range(HALVES):
+                first_product(1, t, u)
+                nc.scalar.activation(h[t][:, u * BANK : (u + 1) * BANK], acc[t, u][:], ACT.Gelu_apprx_tanh)
+
+        w2_bf = keep.tile([P, N, PACK], BF16, name="w2_bf", align_bytes=64)
+        dst, src = interleave_views(w2_bf[:], w2_raw[:])
+        nc.vector.tensor_copy(dst, src)
+        w2_words = keep.tile([P, N], U32, name="w2_words", align_bytes=64)
+        w2_scales = keep.tile([P, N], U8, name="w2_scales", align_bytes=64)
+
+        terms = {}
+        fetched = {}
+        for s, (v0, v1) in enumerate(V_SLICES):
+            for d in range(2):
+                terms[s, d] = keep.tile([P, PACK, v1 - v0], F32, name=f"terms{s}_{d}")
+
+        def fused_term(t, s, d):
+            v0, v1 = V_SLICES[s]
+            nc.vector.tensor_tensor(
+                terms[s, d][:, t, :], h[t][:].indirect(entries(pos_sb[d], v0, v1)), gate_sb[:, d, v0:v1], MULT
+            )
+
+        def fetch(t, s, d):
+            v0, v1 = V_SLICES[s]
+            fetched[t, s, d] = keep.tile([P, v1 - v0], F32, name=f"fetched{t}_{s}_{d}")
+            nc.scalar.activation(fetched[t, s, d][:], h[t][:].indirect(entries(pos_sb[d], v0, v1)), ACT.Copy)
+
+        def weigh(t, s, d):
+            v0, v1 = V_SLICES[s]
+            nc.vector.tensor_tensor(terms[s, d][:, t, :], fetched[t, s, d][:], gate_sb[:, d, v0:v1], MULT)
+
+        z_bf = {}
+
+        def add_terms(s):
+            v0, v1 = V_SLICES[s]
+            z_bf[s] = keep.tile([P, v1 - v0, PACK], BF16, name=f"z_bf{s}", align_bytes=64)
+            dst, first = interleave_views(z_bf[s][:], terms[s, 0][:])
+            second = terms[s, 1][:].rearrange("p j (c i) -> p c j i", i=4)
+            nc.vector.tensor_tensor(dst, first, second, ADD)
+
         g_sb = [keep.tile([P, V], F32, name=f"g{b}") for b in range(G_TILES)]
 
-        def second_product(s, spans):
-            base, end = spans[0][0], spans[-1][1]
-            banks = [psum.tile([P, BANK], F32, name=f"g_acc{s}_{b}", tag=f"bank{2 * s + b}") for b in range(G_TILES)]
-            for v0, v1 in spans:
-                words, scales = late_words[:, N + v0 : N + v1], late_scales[:, N + v0 : N + v1]
-                quantize(words, scales, z_bf[s][:, (v0 - base) * PACK : (v1 - base) * PACK])
-                for b in range(G_TILES):
-                    nc.tensor.matmul_mx(
-                        out=banks[b][:, v0 - base : v1 - base],
-                        lhsT=late_words[:, b * P : (b + 1) * P].bitcast(FP8X4),
-                        lhsT_scale=late_scales[:, b * P : (b + 1) * P],
-                        rhs=words.bitcast(FP8X4),
-                        rhs_scale=scales,
-                        start=True,
-                        stop=True,
-                    )
+        def second_product(s):
+            v0, v1 = V_SLICES[s]
+            words = keep.tile([P, v1 - v0], U32, name=f"z_words{s}", align_bytes=64)
+            scales = keep.tile([P, v1 - v0], U8, name=f"z_scales{s}", align_bytes=64)
+            quantize(words[:], scales[:], z_bf[s][:].rearrange("p c j -> p (c j)"))
             for b in range(G_TILES):
-                if s == 0 and b == 1:
-                    nc.vector.tensor_scalar_max(g_sb[b][:, base:end], banks[b][:, : end - base], 0.0)
+                bank = psum.tile([P, v1 - v0], F32, name=f"g_acc{s}_{b}", tag=f"bank{2 * s + b}")
+                nc.tensor.matmul_mx(
+                    out=bank[:],
+                    lhsT=w2_words[:, b * P : (b + 1) * P].bitcast(FP8X4),
+                    lhsT_scale=w2_scales[:, b * P : (b + 1) * P],
+                    rhs=words[:].bitcast(FP8X4),
+                    rhs_scale=scales[:],
+                    start=True,
+                    stop=True,
+                )
+                if s == len(V_SLICES) - 1 and b == 0:
+                    nc.vector.tensor_scalar_max(g_sb[b][:, v0:v1], bank[:], 0.0)
                 else:
-                    nc.scalar.activation(g_sb[b][:, base:end], banks[b][:, : end - base], ACT.Relu)
+                    nc.scalar.activation(g_sb[b][:, v0:v1], bank[:], ACT.Relu)
 
-        second_product(0, [(0, 256), (256, V_SPLIT)])
-        turn_back(z_rows, 0, 1, z_bf[1], 6, nc.vector.tensor_copy)
-        second_product(1, [(V_SPLIT, V)])
-
-        for b in range(G_TILES):
-            pair = keep.tile([P, 2, U], F32, name=f"pair{b}")
+        for s in range(2):
             for d in range(2):
-                nc.vector.tensor_tensor(pair[:, d, :], g_sb[b][:].indirect(nxt_sb[d][:]), gate2_sb[:, d, :], MULT)
-            result = keep.tile([P, U], F32, name=f"result{b}")
-            nc.vector.tensor_tensor(result[:], pair[:, 0, :], pair[:, 1, :], ADD)
-            nc.sync.dma_start(out[b * P : (b + 1) * P, :], result[:])
+                fused_term(0, s, d)
+        quantize(w2_words[:], w2_scales[:], w2_bf[:].rearrange("p c j -> p (c j)"))
+        for s in range(2):
+            for d in range(2):
+                fused_term(1, s, d)
+        for s in range(2):
+            for t in (2, 3):
+                for d in range(2):
+                    fetch(t, s, d)
+        for t in (2, 3):
+            for d in range(2):
+                weigh(t, 0, d)
+        add_terms(0)
+        for d in range(2):
+            weigh(2, 1, d)
+        second_product(0)
+        for d in range(2):
+            weigh(3, 1, d)
+        add_terms(1)
+        second_product(1)
+
+        pair = [keep.tile([P, 2, U], F32, name=f"pair{b}") for b in range(G_TILES)]
+        result = [keep.tile([P, U], F32, name=f"result{b}") for b in range(G_TILES)]
+        plain = keep.tile([P, 2, U], F32, name="plain")
+        for d in range(2):
+            nc.vector.tensor_tensor(pair[0][:, d, :], g_sb[0][:].indirect(nxt_sb[d][:]), gate2_sb[:, d, :], MULT)
+            nc.scalar.activation(plain[:, d, :], g_sb[1][:].indirect(nxt_sb[d][:]), ACT.Copy)
+        nc.vector.tensor_tensor(pair[1][:, 0, :], plain[:, 0, :], gate2_sb[:, 0, :], MULT)
+        nc.vector.tensor_tensor(result[0][:], pair[0][:, 0, :], pair[0][:, 1, :], ADD)
+        nc.sync.dma_start(out[0:P, :], result[0][:])
+        nc.vector.tensor_tensor(pair[1][:, 1, :], plain[:, 1, :], gate2_sb[:, 1, :], MULT)
+        nc.vector.tensor_tensor(result[1][:], pair[1][:, 0, :], pair[1][:, 1, :], ADD)
+        nc.sync.dma_start(out[P : 2 * P, :], result[1][:])

@@ -23,8 +23,8 @@ BANK = 512
 HALVES = S // BANK
 G_TILES = N // P
 VECTOR_ENTRIES = 384
-VECTOR_ENTRIES_LAST = 256
-V_SLICES = [(0, 256), (256, 512)]
+VECTOR_ENTRIES_LAST = 320
+V_SLICES = [(0, 256), (256, 384), (384, 512)]
 
 
 def interleave_views(dst, src):
@@ -65,17 +65,15 @@ def tile_picked_hop2_gelu_e_kernel(tc, xT, w1, w2, gate, gate2, offs, pos1, pos2
 
         planes = {(0, 0): load_plane(0, 0)}
         offs_sb = load_list("offs_sb", offs)
-        for n in range(1, PASSES * PACK - 1):
+        for n in range(1, PASSES * PACK):
             planes[n // PACK, n % PACK] = load_plane(n // PACK, n % PACK)
-        w1_raw = [load_w1(0)]
-        planes[1, 3] = load_plane(1, 3)
-        w1_raw.append(load_w1(1))
+        w1_raw = [load_w1(g) for g in range(PASSES)]
         pos_sb = [load_list("pos1_sb", pos1), load_list("pos2_sb", pos2)]
-        gate_sb = keep.tile([P, 2, V], F32, name="gate_sb")
-        nc.sync.dma_start(gate_sb[:], gate.rearrange("d p v -> p d v"))
         w2_raw = keep.tile([P, PACK, N], F32, name="w2_raw")
         for t in range(PACK):
             nc.sync.dma_start(w2_raw[:, t, :], w2.rearrange("(a t r) n -> t a r n", t=PACK, r=4)[t])
+        gate_sb = keep.tile([P, 2, V], F32, name="gate_sb")
+        nc.sync.dma_start(gate_sb[:], gate.rearrange("d p v -> p d v"))
         gate2_sb = keep.tile([P, 2, U], F32, name="gate2_sb")
         nc.sync.dma_start(gate2_sb[:], gate2.rearrange("d p v -> p d v"))
         nxt_sb = [load_list("nxt1_sb", nxt1), load_list("nxt2_sb", nxt2)]
@@ -88,7 +86,6 @@ def tile_picked_hop2_gelu_e_kernel(tc, xT, w1, w2, gate, gate2, offs, pos1, pos2
             for u in range(HALVES):
                 picked[g, u] = keep.tile([P, PACK, BANK], F32, name=f"picked{g}_{u}")
                 x_bf[g, u] = keep.tile([P, BANK, PACK], BF16, name=f"x_bf{g}_{u}", align_bytes=64)
-                x_words[g, u] = keep.tile([P, BANK], U32, name=f"x_words{g}_{u}", align_bytes=64)
                 x_scales[g, u] = keep.tile([P, BANK], U8, name=f"x_scales{g}_{u}", align_bytes=64)
 
         def gather_plane(g, j, cut):
@@ -101,32 +98,35 @@ def tile_picked_hop2_gelu_e_kernel(tc, xT, w1, w2, gate, gate2, offs, pos1, pos2
             dst, src = interleave_views(x_bf[g, u][:], picked[g, u][:])
             nc.vector.tensor_copy(dst, src)
 
-        def quantize_x(g, u):
+        def quantize_x(g, u, tag):
+            x_words[g, u] = keep.tile([P, BANK], U32, name=f"x_words{g}_{u}", tag=tag, align_bytes=64)
             quantize(x_words[g, u][:], x_scales[g, u][:], x_bf[g, u][:].rearrange("p c j -> p (c j)"))
 
-        w1_bf, w1_words, w1_scales = {}, {}, {}
+        w1_words, w1_scales = {}, {}
 
-        def round_w1(g, t0, t1, copy):
-            grouped = keep.tile([P, t1 - t0, P, PACK], BF16, name=f"w1_bf{g}_{t0}", align_bytes=64)
+        def w1_tile(name, count, tag):
+            return keep.tile([P, count, P, PACK], BF16, name=name, tag=tag, align_bytes=64)
+
+        def round_w1(grouped, g, t0, t1, copy):
             copy(
-                grouped[:].rearrange("p t (a r) j -> p t a j r", r=4),
+                grouped.rearrange("p t (a r) j -> p t a j r", r=4),
                 w1_raw[g][:].rearrange("p j (a t r) -> p t a j r", t=PACK, r=4)[:, t0:t1],
             )
-            w1_bf[g, t0] = grouped
 
-        def quantize_w1(g, t0, t1):
-            words = keep.tile([P, (t1 - t0) * P], U32, name=f"w1_words{g}_{t0}", align_bytes=64)
-            scales = keep.tile([P, (t1 - t0) * P], U8, name=f"w1_scales{g}_{t0}", align_bytes=64)
-            quantize(words[:], scales[:], w1_bf[g, t0][:].rearrange("p t m j -> p (t m j)"))
-            for t in range(t0, t1):
-                w1_words[g, t] = words[:, (t - t0) * P : (t - t0 + 1) * P]
-                w1_scales[g, t] = scales[:, (t - t0) * P : (t - t0 + 1) * P]
+        def quantize_w1(grouped, parts):
+            g, t = parts[0]
+            words = keep.tile([P, len(parts) * P], U32, name=f"w1_words{g}_{t}", align_bytes=64)
+            scales = keep.tile([P, len(parts) * P], U8, name=f"w1_scales{g}_{t}", align_bytes=64)
+            quantize(words[:], scales[:], grouped.rearrange("p t m j -> p (t m j)"))
+            for n, part in enumerate(parts):
+                w1_words[part] = words[:, n * P : (n + 1) * P]
+                w1_scales[part] = scales[:, n * P : (n + 1) * P]
 
         acc = {}
 
         def first_product(g, t, u):
             if g == 0:
-                acc[t, u] = psum.tile([P, BANK], F32, name=f"acc{t}_{u}", tag=f"bank{2 * t + u}")
+                acc[t, u] = psum.tile([P, BANK], F32, name=f"acc{t}_{u}", tag=f"bank{(2 * t + u) % 3}")
             nc.tensor.matmul_mx(
                 out=acc[t, u][:],
                 lhsT=w1_words[g, t].bitcast(FP8X4),
@@ -141,32 +141,38 @@ def tile_picked_hop2_gelu_e_kernel(tc, xT, w1, w2, gate, gate2, offs, pos1, pos2
             gather_plane(0, j, VECTOR_ENTRIES)
         interleave_x(0, 0)
         gather_plane(1, 0, VECTOR_ENTRIES)
-        quantize_x(0, 0)
+        quantize_x(0, 0, "x_words0_0")
         interleave_x(0, 1)
         gather_plane(1, 1, VECTOR_ENTRIES)
-        quantize_x(0, 1)
+        quantize_x(0, 1, "x_words0_1")
         gather_plane(1, 2, VECTOR_ENTRIES)
-        round_w1(0, 0, 2, nc.vector.tensor_copy)
-        round_w1(0, 2, 4, nc.scalar.copy)
-        quantize_w1(0, 0, 2)
-        quantize_w1(0, 2, 4)
-        for t in range(PACK):
-            for u in range(HALVES):
-                first_product(0, t, u)
         gather_plane(1, 3, VECTOR_ENTRIES_LAST)
         interleave_x(1, 0)
         interleave_x(1, 1)
-        quantize_x(1, 0)
-        for t in range(PACK):
-            round_w1(1, t, t + 1, nc.scalar.copy)
-        quantize_w1(1, 0, 1)
-        quantize_x(1, 1)
-        for t in range(1, PACK):
-            quantize_w1(1, t, t + 1)
+        early = [w1_tile(f"w1_early{t}", 1, f"w1_early{t}") for t in range(3)]
+        for t in range(3):
+            round_w1(early[t][:], 0, t, t + 1, nc.scalar.copy)
+        quantize_w1(early[0][:], [(0, 0)])
+        quantize_w1(early[1][:], [(0, 1)])
+        quantize_x(1, 0, "w1_early0")
+        quantize_x(1, 1, "w1_early1")
+        closing = [w1_tile(f"w1_closing{t}", 1, f"w1_closing{t}") for t in range(2)]
+        for t in range(2):
+            round_w1(closing[t][:], 1, t, t + 1, nc.scalar.copy)
+        quantize_w1(closing[0][:], [(1, 0)])
+        quantize_w1(early[2][:], [(0, 2)])
+        late = w1_tile("w1_late", 3, "w1_closing0")
+        round_w1(late[:, 0:2], 1, 2, 4, nc.vector.tensor_copy)
+        round_w1(late[:, 2:3], 0, 3, 4, nc.scalar.copy)
+        quantize_w1(closing[1][:], [(1, 1)])
+        quantize_w1(late[:, 0:1], [(1, 2)])
+        quantize_w1(late[:, 1:3], [(1, 3), (0, 3)])
 
         h = [keep.tile([P, S], F32, name=f"h{t}") for t in range(PACK)]
+
         for t in range(PACK):
             for u in range(HALVES):
+                first_product(0, t, u)
                 first_product(1, t, u)
                 nc.scalar.activation(h[t][:, u * BANK : (u + 1) * BANK], acc[t, u][:], ACT.Gelu_apprx_tanh)
 
@@ -188,14 +194,16 @@ def tile_picked_hop2_gelu_e_kernel(tc, xT, w1, w2, gate, gate2, offs, pos1, pos2
                 terms[s, d][:, t, :], h[t][:].indirect(entries(pos_sb[d], v0, v1)), gate_sb[:, d, v0:v1], MULT
             )
 
-        def fetch(t, s, d):
+        def fetch(t0, s, d):
             v0, v1 = V_SLICES[s]
-            fetched[t, s, d] = keep.tile([P, v1 - v0], F32, name=f"fetched{t}_{s}_{d}")
-            nc.scalar.activation(fetched[t, s, d][:], h[t][:].indirect(entries(pos_sb[d], v0, v1)), ACT.Copy)
+            fetched[s, d] = keep.tile([P, PACK - t0, v1 - v0], F32, name=f"fetched{s}_{d}")
+            for t in range(t0, PACK):
+                nc.scalar.activation(fetched[s, d][:, t - t0, :], h[t][:].indirect(entries(pos_sb[d], v0, v1)), ACT.Copy)
 
-        def weigh(t, s, d):
+        def weigh(first, s, d, t0, t1):
             v0, v1 = V_SLICES[s]
-            nc.vector.tensor_tensor(terms[s, d][:, t, :], fetched[t, s, d][:], gate_sb[:, d, v0:v1], MULT)
+            weights = gate_sb[:, d : d + 1, v0:v1].to_broadcast([P, t1 - t0, v1 - v0])
+            nc.vector.tensor_tensor(terms[s, d][:, t0:t1, :], fetched[s, d][:, t0 - first : t1 - first, :], weights, MULT)
 
         z_bf = {}
 
@@ -214,7 +222,7 @@ def tile_picked_hop2_gelu_e_kernel(tc, xT, w1, w2, gate, gate2, offs, pos1, pos2
             scales = keep.tile([P, v1 - v0], U8, name=f"z_scales{s}", align_bytes=64)
             quantize(words[:], scales[:], z_bf[s][:].rearrange("p c j -> p (c j)"))
             for b in range(G_TILES):
-                bank = psum.tile([P, v1 - v0], F32, name=f"g_acc{s}_{b}", tag=f"bank{2 * s + b}")
+                bank = psum.tile([P, v1 - v0], F32, name=f"g_acc{s}_{b}", tag=f"bank{4 + (2 * s + b) % 4}")
                 nc.tensor.matmul_mx(
                     out=bank[:],
                     lhsT=w2_words[:, b * P : (b + 1) * P].bitcast(FP8X4),
@@ -229,38 +237,36 @@ def tile_picked_hop2_gelu_e_kernel(tc, xT, w1, w2, gate, gate2, offs, pos1, pos2
                 else:
                     nc.scalar.activation(g_sb[b][:, v0:v1], bank[:], ACT.Relu)
 
-        for s in range(2):
-            for d in range(2):
-                fused_term(0, s, d)
         quantize(w2_words[:], w2_scales[:], w2_bf[:].rearrange("p c j -> p (c j)"))
-        for s in range(2):
+        for t in range(PACK):
             for d in range(2):
-                fused_term(1, s, d)
-        for s in range(2):
-            for t in (2, 3):
-                for d in range(2):
-                    fetch(t, s, d)
-        for t in (2, 3):
-            for d in range(2):
-                weigh(t, 0, d)
+                fused_term(t, 0, d)
+            if t == 0:
+                fused_term(0, 1, 0)
+        fetch(1, 1, 0)
+        fetch(0, 1, 1)
+        fetch(0, 2, 0)
+        fetch(0, 2, 1)
+        weigh(1, 1, 0, 1, PACK)
         add_terms(0)
-        for d in range(2):
-            weigh(2, 1, d)
+        weigh(0, 1, 1, 0, PACK)
         second_product(0)
-        for d in range(2):
-            weigh(3, 1, d)
         add_terms(1)
+        weigh(0, 2, 0, 0, PACK)
+        weigh(0, 2, 1, 0, 2)
         second_product(1)
+        weigh(0, 2, 1, 2, PACK)
+        add_terms(2)
+        second_product(2)
 
         pair = [keep.tile([P, 2, U], F32, name=f"pair{b}") for b in range(G_TILES)]
         result = [keep.tile([P, U], F32, name=f"result{b}") for b in range(G_TILES)]
-        plain = keep.tile([P, 2, U], F32, name="plain")
-        for d in range(2):
-            nc.vector.tensor_tensor(pair[0][:, d, :], g_sb[0][:].indirect(nxt_sb[d][:]), gate2_sb[:, d, :], MULT)
-            nc.scalar.activation(plain[:, d, :], g_sb[1][:].indirect(nxt_sb[d][:]), ACT.Copy)
-        nc.vector.tensor_tensor(pair[1][:, 0, :], plain[:, 0, :], gate2_sb[:, 0, :], MULT)
-        nc.vector.tensor_tensor(result[0][:], pair[0][:, 0, :], pair[0][:, 1, :], ADD)
-        nc.sync.dma_start(out[0:P, :], result[0][:])
-        nc.vector.tensor_tensor(pair[1][:, 1, :], plain[:, 1, :], gate2_sb[:, 1, :], MULT)
-        nc.vector.tensor_tensor(result[1][:], pair[1][:, 0, :], pair[1][:, 1, :], ADD)
-        nc.sync.dma_start(out[P : 2 * P, :], result[1][:])
+        plain = [keep.tile([P, U], F32, name=f"plain{b}") for b in range(G_TILES)]
+        for b in range(G_TILES):
+            nc.vector.tensor_tensor(pair[b][:, 0, :], g_sb[b][:].indirect(nxt_sb[0][:]), gate2_sb[:, 0, :], MULT)
+            nc.scalar.activation(plain[b][:], g_sb[b][:].indirect(nxt_sb[1][:]), ACT.Copy)
+        for b in range(G_TILES):
+            nc.vector.tensor_tensor(pair[b][:, 1, :], plain[b][:], gate2_sb[:, 1, :], MULT)
+        for b in range(G_TILES):
+            nc.vector.tensor_tensor(result[b][:], pair[b][:, 0, :], pair[b][:, 1, :], ADD)
+            nc.sync.dma_start(out[b * P : (b + 1) * P, :], result[b][:])

@@ -24,7 +24,7 @@ HALVES = S // BANK
 G_TILES = N // P
 VECTOR_ENTRIES = 384
 VECTOR_ENTRIES_LAST = 320
-V_SLICES = [(0, 256), (256, 384), (384, 512)]
+V_SLICES = [(0, 256), (256, 448), (448, 512)]
 
 
 def interleave_views(dst, src):
@@ -210,9 +210,8 @@ def tile_picked_hop2_gelu_e_kernel(tc, xT, w1, w2, gate, gate2, offs, pos1, pos2
         def add_terms(s):
             v0, v1 = V_SLICES[s]
             z_bf[s] = keep.tile([P, v1 - v0, PACK], BF16, name=f"z_bf{s}", align_bytes=64)
-            dst, first = interleave_views(z_bf[s][:], terms[s, 0][:])
-            second = terms[s, 1][:].rearrange("p j (c i) -> p c j i", i=4)
-            nc.vector.tensor_tensor(dst, first, second, ADD)
+            first, second = [terms[s, d][:].rearrange("p j (c i) -> p c j i", i=2) for d in range(2)]
+            nc.vector.tensor_tensor(z_bf[s][:].rearrange("p (c i) j -> p c j i", i=2), first, second, ADD)
 
         g_sb = [keep.tile([P, V], F32, name=f"g{b}") for b in range(G_TILES)]
 
@@ -220,18 +219,21 @@ def tile_picked_hop2_gelu_e_kernel(tc, xT, w1, w2, gate, gate2, offs, pos1, pos2
             v0, v1 = V_SLICES[s]
             words = keep.tile([P, v1 - v0], U32, name=f"z_words{s}", align_bytes=64)
             scales = keep.tile([P, v1 - v0], U8, name=f"z_scales{s}", align_bytes=64)
-            quantize(words[:], scales[:], z_bf[s][:].rearrange("p c j -> p (c j)"))
+            pieces = [(0, 128), (128, 192)] if v1 - v0 == 192 else [(0, v1 - v0)]
+            for c0, c1 in pieces:
+                quantize(words[:, c0:c1], scales[:, c0:c1], z_bf[s][:, c0:c1, :].rearrange("p c j -> p (c j)"))
             for b in range(G_TILES):
                 bank = psum.tile([P, v1 - v0], F32, name=f"g_acc{s}_{b}", tag=f"bank{4 + (2 * s + b) % 4}")
-                nc.tensor.matmul_mx(
-                    out=bank[:],
-                    lhsT=w2_words[:, b * P : (b + 1) * P].bitcast(FP8X4),
-                    lhsT_scale=w2_scales[:, b * P : (b + 1) * P],
-                    rhs=words[:].bitcast(FP8X4),
-                    rhs_scale=scales[:],
-                    start=True,
-                    stop=True,
-                )
+                for c0, c1 in pieces:
+                    nc.tensor.matmul_mx(
+                        out=bank[:, c0:c1],
+                        lhsT=w2_words[:, b * P : (b + 1) * P].bitcast(FP8X4),
+                        lhsT_scale=w2_scales[:, b * P : (b + 1) * P],
+                        rhs=words[:, c0:c1].bitcast(FP8X4),
+                        rhs_scale=scales[:, c0:c1],
+                        start=True,
+                        stop=True,
+                    )
                 if s == len(V_SLICES) - 1 and b == 0:
                     nc.vector.tensor_scalar_max(g_sb[b][:, v0:v1], bank[:], 0.0)
                 else:
@@ -253,9 +255,8 @@ def tile_picked_hop2_gelu_e_kernel(tc, xT, w1, w2, gate, gate2, offs, pos1, pos2
         second_product(0)
         add_terms(1)
         weigh(0, 2, 0, 0, PACK)
-        weigh(0, 2, 1, 0, 2)
+        weigh(0, 2, 1, 0, PACK)
         second_product(1)
-        weigh(0, 2, 1, 2, PACK)
         add_terms(2)
         second_product(2)
 

@@ -17,14 +17,21 @@ ADD = mybir.AluOpType.add
 
 P = 128
 PACK = 4
+RUN = 4
+LIST_ROWS = 16
 K_PASS = P * PACK
 PASSES = K // K_PASS
 BANK = 512
 HALVES = S // BANK
 G_TILES = N // P
+NEIGHBOURS = 2
+
 VECTOR_ENTRIES = 384
 VECTOR_ENTRIES_LAST = 320
+H_BANKS = 3
+G_BANK0, G_BANKS = 4, 4
 V_SLICES = [(0, 256), (256, 448), (448, 512)]
+V_PIECES = [[(0, 256)], [(0, 128), (128, 192)], [(0, 64)]]
 
 
 def interleave_views(dst, src):
@@ -32,7 +39,7 @@ def interleave_views(dst, src):
 
 
 def entries(offsets, e0, e1):
-    return offsets[:, e0 // 16 : e1 // 16]
+    return offsets[:, e0 // LIST_ROWS : e1 // LIST_ROWS]
 
 
 def tile_picked_hop2_gelu_e_kernel(tc, xT, w1, w2, gate, gate2, offs, pos1, pos2, nxt1, nxt2, out):
@@ -71,17 +78,14 @@ def tile_picked_hop2_gelu_e_kernel(tc, xT, w1, w2, gate, gate2, offs, pos1, pos2
         pos_sb = [load_list("pos1_sb", pos1), load_list("pos2_sb", pos2)]
         w2_raw = keep.tile([P, PACK, N], F32, name="w2_raw")
         for t in range(PACK):
-            nc.sync.dma_start(w2_raw[:, t, :], w2.rearrange("(a t r) n -> t a r n", t=PACK, r=4)[t])
-        gate_sb = keep.tile([P, 2, V], F32, name="gate_sb")
+            nc.sync.dma_start(w2_raw[:, t, :], w2.rearrange("(a t r) n -> t a r n", t=PACK, r=RUN)[t])
+        gate_sb = keep.tile([P, NEIGHBOURS, V], F32, name="gate_sb")
         nc.sync.dma_start(gate_sb[:], gate.rearrange("d p v -> p d v"))
-        gate2_sb = keep.tile([P, 2, U], F32, name="gate2_sb")
+        gate2_sb = keep.tile([P, NEIGHBOURS, U], F32, name="gate2_sb")
         nc.sync.dma_start(gate2_sb[:], gate2.rearrange("d p v -> p d v"))
         nxt_sb = [load_list("nxt1_sb", nxt1), load_list("nxt2_sb", nxt2)]
 
-        picked = {}
-        x_bf = {}
-        x_words = {}
-        x_scales = {}
+        picked, x_bf, x_words, x_scales = {}, {}, {}, {}
         for g in range(PASSES):
             for u in range(HALVES):
                 picked[g, u] = keep.tile([P, PACK, BANK], F32, name=f"picked{g}_{u}")
@@ -109,8 +113,8 @@ def tile_picked_hop2_gelu_e_kernel(tc, xT, w1, w2, gate, gate2, offs, pos1, pos2
 
         def round_w1(grouped, g, t0, t1, copy):
             copy(
-                grouped.rearrange("p t (a r) j -> p t a j r", r=4),
-                w1_raw[g][:].rearrange("p j (a t r) -> p t a j r", t=PACK, r=4)[:, t0:t1],
+                grouped.rearrange("p t (a r) j -> p t a j r", r=RUN),
+                w1_raw[g][:].rearrange("p j (a t r) -> p t a j r", t=PACK, r=RUN)[:, t0:t1],
             )
 
         def quantize_w1(grouped, parts):
@@ -122,40 +126,24 @@ def tile_picked_hop2_gelu_e_kernel(tc, xT, w1, w2, gate, gate2, offs, pos1, pos2
                 w1_words[part] = words[:, n * P : (n + 1) * P]
                 w1_scales[part] = scales[:, n * P : (n + 1) * P]
 
-        acc = {}
-
-        def first_product(g, t, u):
-            if g == 0:
-                acc[t, u] = psum.tile([P, BANK], F32, name=f"acc{t}_{u}", tag=f"bank{(2 * t + u) % 3}")
-            nc.tensor.matmul_mx(
-                out=acc[t, u][:],
-                lhsT=w1_words[g, t].bitcast(FP8X4),
-                lhsT_scale=w1_scales[g, t],
-                rhs=x_words[g, u][:].bitcast(FP8X4),
-                rhs_scale=x_scales[g, u][:],
-                start=(g == 0),
-                stop=(g == PASSES - 1),
-            )
-
         for j in range(PACK):
             gather_plane(0, j, VECTOR_ENTRIES)
-        interleave_x(0, 0)
-        gather_plane(1, 0, VECTOR_ENTRIES)
-        quantize_x(0, 0, "x_words0_0")
-        interleave_x(0, 1)
-        gather_plane(1, 1, VECTOR_ENTRIES)
-        quantize_x(0, 1, "x_words0_1")
+        for u in range(HALVES):
+            interleave_x(0, u)
+            gather_plane(1, u, VECTOR_ENTRIES)
+            quantize_x(0, u, f"x_words0_{u}")
         gather_plane(1, 2, VECTOR_ENTRIES)
         gather_plane(1, 3, VECTOR_ENTRIES_LAST)
-        interleave_x(1, 0)
-        interleave_x(1, 1)
-        early = [w1_tile(f"w1_early{t}", 1, f"w1_early{t}") for t in range(3)]
-        for t in range(3):
+        for u in range(HALVES):
+            interleave_x(1, u)
+
+        early = [w1_tile(f"w1_early{t}", 1, f"w1_early{t}") for t in range(PACK - 1)]
+        for t in range(PACK - 1):
             round_w1(early[t][:], 0, t, t + 1, nc.scalar.copy)
-        quantize_w1(early[0][:], [(0, 0)])
-        quantize_w1(early[1][:], [(0, 1)])
-        quantize_x(1, 0, "w1_early0")
-        quantize_x(1, 1, "w1_early1")
+        for u in range(HALVES):
+            quantize_w1(early[u][:], [(0, u)])
+        for u in range(HALVES):
+            quantize_x(1, u, f"w1_early{u}")
         closing = [w1_tile(f"w1_closing{t}", 1, f"w1_closing{t}") for t in range(2)]
         for t in range(2):
             round_w1(closing[t][:], 1, t, t + 1, nc.scalar.copy)
@@ -169,12 +157,20 @@ def tile_picked_hop2_gelu_e_kernel(tc, xT, w1, w2, gate, gate2, offs, pos1, pos2
         quantize_w1(late[:, 1:3], [(1, 3), (0, 3)])
 
         h = [keep.tile([P, S], F32, name=f"h{t}") for t in range(PACK)]
-
         for t in range(PACK):
             for u in range(HALVES):
-                first_product(0, t, u)
-                first_product(1, t, u)
-                nc.scalar.activation(h[t][:, u * BANK : (u + 1) * BANK], acc[t, u][:], ACT.Gelu_apprx_tanh)
+                acc = psum.tile([P, BANK], F32, name=f"acc{t}_{u}", tag=f"bank{(HALVES * t + u) % H_BANKS}")
+                for g in range(PASSES):
+                    nc.tensor.matmul_mx(
+                        out=acc[:],
+                        lhsT=w1_words[g, t].bitcast(FP8X4),
+                        lhsT_scale=w1_scales[g, t],
+                        rhs=x_words[g, u][:].bitcast(FP8X4),
+                        rhs_scale=x_scales[g, u][:],
+                        start=(g == 0),
+                        stop=(g == PASSES - 1),
+                    )
+                nc.scalar.activation(h[t][:, u * BANK : (u + 1) * BANK], acc[:], ACT.Gelu_apprx_tanh)
 
         w2_bf = keep.tile([P, N, PACK], BF16, name="w2_bf", align_bytes=64)
         dst, src = interleave_views(w2_bf[:], w2_raw[:])
@@ -182,10 +178,9 @@ def tile_picked_hop2_gelu_e_kernel(tc, xT, w1, w2, gate, gate2, offs, pos1, pos2
         w2_words = keep.tile([P, N], U32, name="w2_words", align_bytes=64)
         w2_scales = keep.tile([P, N], U8, name="w2_scales", align_bytes=64)
 
-        terms = {}
-        fetched = {}
+        terms, fetched, z_bf = {}, {}, {}
         for s, (v0, v1) in enumerate(V_SLICES):
-            for d in range(2):
+            for d in range(NEIGHBOURS):
                 terms[s, d] = keep.tile([P, PACK, v1 - v0], F32, name=f"terms{s}_{d}")
 
         def fused_term(t, s, d):
@@ -194,24 +189,22 @@ def tile_picked_hop2_gelu_e_kernel(tc, xT, w1, w2, gate, gate2, offs, pos1, pos2
                 terms[s, d][:, t, :], h[t][:].indirect(entries(pos_sb[d], v0, v1)), gate_sb[:, d, v0:v1], MULT
             )
 
-        def fetch(t0, s, d):
+        def fetch(s, d, t0):
             v0, v1 = V_SLICES[s]
             fetched[s, d] = keep.tile([P, PACK - t0, v1 - v0], F32, name=f"fetched{s}_{d}")
             for t in range(t0, PACK):
                 nc.scalar.activation(fetched[s, d][:, t - t0, :], h[t][:].indirect(entries(pos_sb[d], v0, v1)), ACT.Copy)
 
-        def weigh(first, s, d, t0, t1):
+        def weigh(s, d, t0):
             v0, v1 = V_SLICES[s]
-            weights = gate_sb[:, d : d + 1, v0:v1].to_broadcast([P, t1 - t0, v1 - v0])
-            nc.vector.tensor_tensor(terms[s, d][:, t0:t1, :], fetched[s, d][:, t0 - first : t1 - first, :], weights, MULT)
-
-        z_bf = {}
+            weights = gate_sb[:, d : d + 1, v0:v1].to_broadcast([P, PACK - t0, v1 - v0])
+            nc.vector.tensor_tensor(terms[s, d][:, t0:, :], fetched[s, d][:], weights, MULT)
 
         def add_terms(s):
             v0, v1 = V_SLICES[s]
             z_bf[s] = keep.tile([P, v1 - v0, PACK], BF16, name=f"z_bf{s}", align_bytes=64)
-            first, second = [terms[s, d][:].rearrange("p j (c i) -> p c j i", i=2) for d in range(2)]
-            nc.vector.tensor_tensor(z_bf[s][:].rearrange("p (c i) j -> p c j i", i=2), first, second, ADD)
+            first, second = [terms[s, d][:].rearrange("p t (c i) -> p c t i", i=2) for d in range(NEIGHBOURS)]
+            nc.vector.tensor_tensor(z_bf[s][:].rearrange("p (c i) t -> p c t i", i=2), first, second, ADD)
 
         g_sb = [keep.tile([P, V], F32, name=f"g{b}") for b in range(G_TILES)]
 
@@ -219,12 +212,12 @@ def tile_picked_hop2_gelu_e_kernel(tc, xT, w1, w2, gate, gate2, offs, pos1, pos2
             v0, v1 = V_SLICES[s]
             words = keep.tile([P, v1 - v0], U32, name=f"z_words{s}", align_bytes=64)
             scales = keep.tile([P, v1 - v0], U8, name=f"z_scales{s}", align_bytes=64)
-            pieces = [(0, 128), (128, 192)] if v1 - v0 == 192 else [(0, v1 - v0)]
-            for c0, c1 in pieces:
-                quantize(words[:, c0:c1], scales[:, c0:c1], z_bf[s][:, c0:c1, :].rearrange("p c j -> p (c j)"))
+            for c0, c1 in V_PIECES[s]:
+                quantize(words[:, c0:c1], scales[:, c0:c1], z_bf[s][:, c0:c1, :].rearrange("p c t -> p (c t)"))
             for b in range(G_TILES):
-                bank = psum.tile([P, v1 - v0], F32, name=f"g_acc{s}_{b}", tag=f"bank{4 + (2 * s + b) % 4}")
-                for c0, c1 in pieces:
+                tag = f"bank{G_BANK0 + (G_TILES * s + b) % G_BANKS}"
+                bank = psum.tile([P, v1 - v0], F32, name=f"g_acc{s}_{b}", tag=tag)
+                for c0, c1 in V_PIECES[s]:
                     nc.tensor.matmul_mx(
                         out=bank[:, c0:c1],
                         lhsT=w2_words[:, b * P : (b + 1) * P].bitcast(FP8X4),
@@ -234,33 +227,30 @@ def tile_picked_hop2_gelu_e_kernel(tc, xT, w1, w2, gate, gate2, offs, pos1, pos2
                         start=True,
                         stop=True,
                     )
-                if s == len(V_SLICES) - 1 and b == 0:
-                    nc.vector.tensor_scalar_max(g_sb[b][:, v0:v1], bank[:], 0.0)
-                else:
-                    nc.scalar.activation(g_sb[b][:, v0:v1], bank[:], ACT.Relu)
+                nc.scalar.activation(g_sb[b][:, v0:v1], bank[:], ACT.Relu)
 
-        quantize(w2_words[:], w2_scales[:], w2_bf[:].rearrange("p c j -> p (c j)"))
+        quantize(w2_words[:], w2_scales[:], w2_bf[:].rearrange("p c t -> p (c t)"))
         for t in range(PACK):
-            for d in range(2):
+            for d in range(NEIGHBOURS):
                 fused_term(t, 0, d)
             if t == 0:
                 fused_term(0, 1, 0)
+        fetch(1, 0, 1)
         fetch(1, 1, 0)
-        fetch(0, 1, 1)
-        fetch(0, 2, 0)
-        fetch(0, 2, 1)
-        weigh(1, 1, 0, 1, PACK)
+        fetch(2, 0, 0)
+        fetch(2, 1, 0)
+        weigh(1, 0, 1)
         add_terms(0)
-        weigh(0, 1, 1, 0, PACK)
+        weigh(1, 1, 0)
         second_product(0)
         add_terms(1)
-        weigh(0, 2, 0, 0, PACK)
-        weigh(0, 2, 1, 0, PACK)
+        weigh(2, 0, 0)
+        weigh(2, 1, 0)
         second_product(1)
         add_terms(2)
         second_product(2)
 
-        pair = [keep.tile([P, 2, U], F32, name=f"pair{b}") for b in range(G_TILES)]
+        pair = [keep.tile([P, NEIGHBOURS, U], F32, name=f"pair{b}") for b in range(G_TILES)]
         result = [keep.tile([P, U], F32, name=f"result{b}") for b in range(G_TILES)]
         plain = [keep.tile([P, U], F32, name=f"plain{b}") for b in range(G_TILES)]
         for b in range(G_TILES):

@@ -23,11 +23,12 @@ K_PASS = P * PACK
 PASSES = K // K_PASS
 BANK = 512
 HALVES = S // BANK
+PAIRS = PASSES * PACK // 2
 G_TILES = N // P
 NEIGHBOURS = 2
 
 VECTOR_ENTRIES = 384
-VECTOR_ENTRIES_LAST = 320
+SCALAR_WEAVES = 128
 H_BANKS = 3
 G_BANK0, G_BANKS = 4, 4
 V_SLICES = [(0, 256), (256, 448), (448, 512)]
@@ -54,13 +55,8 @@ def tile_picked_hop2_gelu_e_kernel(tc, xT, w1, w2, gate, gate2, offs, pos1, pos2
             return tile
 
         def load_plane(g, j):
-            tile = keep.tile([P, T], F32, name=f"x_plane{g}_{j}")
+            tile = keep.tile([P, T], F32, name=f"x_plane{g}_{j}", tag=f"x_plane{g}_{j}", align_bytes=64)
             nc.sync.dma_start(tile[:], xT[g * K_PASS : (g + 1) * K_PASS, :].rearrange("(p j) c -> j p c", j=PACK)[j])
-            return tile
-
-        def load_w1(g):
-            tile = keep.tile([P, PACK, H], F32, name=f"w1_raw{g}")
-            nc.sync.dma_start(tile[:], w1[g * K_PASS : (g + 1) * K_PASS, :].rearrange("(p j) c -> p j c", j=PACK))
             return tile
 
         def quantize(words, scales, values):
@@ -74,87 +70,123 @@ def tile_picked_hop2_gelu_e_kernel(tc, xT, w1, w2, gate, gate2, offs, pos1, pos2
         offs_sb = load_list("offs_sb", offs)
         for n in range(1, PASSES * PACK):
             planes[n // PACK, n % PACK] = load_plane(n // PACK, n % PACK)
-        w1_raw = [load_w1(g) for g in range(PASSES)]
-        pos_sb = [load_list("pos1_sb", pos1), load_list("pos2_sb", pos2)]
+        w1_raw = keep.tile([P, PASSES, PACK, H], F32, name="w1_raw")
+        for g in range(PASSES):
+            nc.sync.dma_start(w1_raw[:, g], w1[g * K_PASS : (g + 1) * K_PASS, :].rearrange("(p j) c -> p j c", j=PACK))
         w2_raw = keep.tile([P, PACK, N], F32, name="w2_raw")
         for t in range(PACK):
             nc.sync.dma_start(w2_raw[:, t, :], w2.rearrange("(a t r) n -> t a r n", t=PACK, r=RUN)[t])
-        gate_sb = keep.tile([P, NEIGHBOURS, V], F32, name="gate_sb")
-        nc.sync.dma_start(gate_sb[:], gate.rearrange("d p v -> p d v"))
+        pos_sb = [load_list("pos1_sb", pos1), load_list("pos2_sb", pos2)]
+        gate_sb = []
+        for v0, v1 in ((0, V // 2), (V // 2, V)):
+            gate_sb.append(keep.tile([P, NEIGHBOURS, v1 - v0], F32, name=f"gate_sb{v0}"))
+            nc.sync.dma_start(gate_sb[-1][:], gate[:, :, v0:v1].rearrange("d p v -> p d v"))
+
+        def gates(d, v0, v1):
+            half = v0 // (V // 2)
+            return gate_sb[half][:, d : d + 1, v0 - half * (V // 2) : v1 - half * (V // 2)]
         gate2_sb = keep.tile([P, NEIGHBOURS, U], F32, name="gate2_sb")
         nc.sync.dma_start(gate2_sb[:], gate2.rearrange("d p v -> p d v"))
         nxt_sb = [load_list("nxt1_sb", nxt1), load_list("nxt2_sb", nxt2)]
 
-        picked, x_bf, x_words, x_scales = {}, {}, {}, {}
-        for g in range(PASSES):
-            for u in range(HALVES):
-                picked[g, u] = keep.tile([P, PACK, BANK], F32, name=f"picked{g}_{u}")
-                x_bf[g, u] = keep.tile([P, BANK, PACK], BF16, name=f"x_bf{g}_{u}", align_bytes=64)
-                x_scales[g, u] = keep.tile([P, BANK], U8, name=f"x_scales{g}_{u}", align_bytes=64)
+        ranges = [[(0, BANK), (BANK, S)], [(0, BANK), (BANK, BANK + SCALAR_WEAVES), (BANK + SCALAR_WEAVES, S)]]
+        x_bf = [
+            {r: keep.tile([P, r[1] - r[0], PACK], BF16, name=f"x_bf{g}_{r[0]}", align_bytes=64) for r in ranges[g]}
+            for g in range(PASSES)
+        ]
+        x_words = {}
+        x_scales = [keep.tile([P, S], U8, name=f"x_scales{g}", align_bytes=64) for g in range(PASSES)]
+        picked = [keep.tile([P, 2, S - VECTOR_ENTRIES], F32, name=f"picked{n}") for n in range(PAIRS)]
 
         def gather_plane(g, j, cut):
             window = planes[g, j][:]
-            nc.vector.tensor_copy(picked[g, 0][:, j, :cut], window.indirect(entries(offs_sb, 0, cut)))
-            nc.scalar.activation(picked[g, 0][:, j, cut:], window.indirect(entries(offs_sb, cut, BANK)), ACT.Copy)
-            nc.scalar.activation(picked[g, 1][:, j, :], window.indirect(entries(offs_sb, BANK, S)), ACT.Copy)
+            nc.vector.tensor_copy(x_bf[g][0, BANK][:, :cut, j], window.indirect(entries(offs_sb, 0, cut)))
+            fetched_part = picked[2 * g + j // 2][:, j % 2, cut - VECTOR_ENTRIES :]
+            nc.scalar.activation(fetched_part, window.indirect(entries(offs_sb, cut, S)), ACT.Copy)
 
-        def interleave_x(g, u):
-            dst, src = interleave_views(x_bf[g, u][:], picked[g, u][:])
-            nc.vector.tensor_copy(dst, src)
+        def interleave_x(n, r, rows, copy):
+            g, j0 = n // 2, 2 * (n % 2)
+            e0 = max(r[0], VECTOR_ENTRIES)
+            source = picked[n][:, :rows, e0 - VECTOR_ENTRIES : r[1] - VECTOR_ENTRIES]
+            copy(*interleave_views(x_bf[g][r][:, e0 - r[0] :, j0 : j0 + rows], source))
 
-        def quantize_x(g, u, tag):
+        def quantize_x(g, r, e0, e1):
+            values = x_bf[g][r][:, e0 - r[0] : e1 - r[0], :].rearrange("p c j -> p (c j)")
+            u = r[0] // BANK
+            quantize(x_words[g, u][:, e0 - u * BANK : e1 - u * BANK], x_scales[g][:, e0:e1], values)
+
+        def words_tile(g, u, tag):
             x_words[g, u] = keep.tile([P, BANK], U32, name=f"x_words{g}_{u}", tag=tag, align_bytes=64)
-            quantize(x_words[g, u][:], x_scales[g, u][:], x_bf[g, u][:].rearrange("p c j -> p (c j)"))
+
+        for n in range(PAIRS - 1):
+            g = n // 2
+            for e in range(2):
+                gather_plane(g, 2 * (n % 2) + e, VECTOR_ENTRIES)
+                if n == 2:
+                    words_tile(0, e, f"x_words0_{e}")
+                    quantize_x(0, ranges[0][e], *ranges[0][e])
+            for r in ranges[g][1:]:
+                interleave_x(n, r, 2, nc.vector.tensor_copy)
+            interleave_x(n, ranges[g][0], 2, nc.scalar.copy)
+        gather_plane(1, 2, VECTOR_ENTRIES)
+        interleave_x(PAIRS - 1, ranges[1][0], 1, nc.vector.tensor_copy)
+        gather_plane(1, 3, BANK)
+        interleave_x(PAIRS - 1, ranges[1][1], 2, nc.scalar.copy)
+        interleave_x(PAIRS - 1, ranges[1][2], 2, nc.vector.tensor_copy)
 
         w1_words, w1_scales = {}, {}
 
-        def w1_tile(name, count, tag):
-            return keep.tile([P, count, P, PACK], BF16, name=name, tag=tag, align_bytes=64)
+        def w1_tile(name, count):
+            return keep.tile([P, count, P, PACK], BF16, name=name, tag=name, align_bytes=64)
 
-        def round_w1(grouped, g, t0, t1, copy):
-            copy(
-                grouped.rearrange("p t (a r) j -> p t a j r", r=RUN),
-                w1_raw[g][:].rearrange("p j (a t r) -> p t a j r", t=PACK, r=RUN)[:, t0:t1],
-            )
+        w1_parts = w1_raw[:].rearrange("p g j (a t r) -> p g t a j r", t=PACK, r=RUN)
 
-        def quantize_w1(grouped, parts):
+        def round_w1(grouped, parts, copy):
+            copy(grouped.rearrange("p n (a r) j -> p n a j r", r=RUN), parts)
+
+        def quantize_w1(grouped, parts, tag=None):
             g, t = parts[0]
-            words = keep.tile([P, len(parts) * P], U32, name=f"w1_words{g}_{t}", align_bytes=64)
+            name = f"w1_words{g}_{t}"
+            words = keep.tile([P, len(parts) * P], U32, name=name, tag=tag or name, align_bytes=64)
             scales = keep.tile([P, len(parts) * P], U8, name=f"w1_scales{g}_{t}", align_bytes=64)
             quantize(words[:], scales[:], grouped.rearrange("p t m j -> p (t m j)"))
             for n, part in enumerate(parts):
                 w1_words[part] = words[:, n * P : (n + 1) * P]
                 w1_scales[part] = scales[:, n * P : (n + 1) * P]
 
-        for j in range(PACK):
-            gather_plane(0, j, VECTOR_ENTRIES)
-        for u in range(HALVES):
-            interleave_x(0, u)
-            gather_plane(1, u, VECTOR_ENTRIES)
-            quantize_x(0, u, f"x_words0_{u}")
-        gather_plane(1, 2, VECTOR_ENTRIES)
-        gather_plane(1, 3, VECTOR_ENTRIES_LAST)
-        for u in range(HALVES):
-            interleave_x(1, u)
+        w00, w01, w10, w13 = [w1_tile(f"w1_bf{g}_{t}", 1) for g, t in ((0, 0), (0, 1), (1, 0), (1, 3))]
+        upper = w1_tile("w1_upper", 2)
+        middle = w1_tile("w1_middle", 2)
+        words_tile(1, 0, f"x_plane{PASSES - 1}_{PACK - 1}")
+        quantize_x(1, ranges[1][0], 0, P)
+        quantize_x(1, ranges[1][0], P, BANK)
+        round_w1(w00[:], w1_parts[:, 0, 0:1], nc.scalar.copy)
+        round_w1(w01[:], w1_parts[:, 0, 1:2], nc.scalar.copy)
+        round_w1(upper[:], w1_parts[:, 0, 2:4], nc.scalar.copy)
+        quantize_w1(w00[:], [(0, 0)])
+        words_tile(1, 1, "w1_bf0_0")
+        for r in ranges[1][1:]:
+            quantize_x(1, r, *r)
+        quantize_w1(w01[:], [(0, 1)])
+        round_w1(w10[:], w1_parts[:, 1, 0:1], nc.vector.tensor_copy)
+        round_w1(w13[:], w1_parts[:, 1, 3:4], nc.vector.tensor_copy)
+        round_w1(middle[:], w1_parts[:, 1, 1:3], nc.scalar.copy)
+        quantize_w1(w10[:], [(1, 0)])
+        quantize_w1(w13[:], [(1, 3)])
+        quantize_w1(upper[:], [(0, 2), (0, 3)], "w1_bf1_0")
+        quantize_w1(middle[:], [(1, 1), (1, 2)])
 
-        early = [w1_tile(f"w1_early{t}", 1, f"w1_early{t}") for t in range(PACK - 1)]
-        for t in range(PACK - 1):
-            round_w1(early[t][:], 0, t, t + 1, nc.scalar.copy)
-        for u in range(HALVES):
-            quantize_w1(early[u][:], [(0, u)])
-        for u in range(HALVES):
-            quantize_x(1, u, f"w1_early{u}")
-        closing = [w1_tile(f"w1_closing{t}", 1, f"w1_closing{t}") for t in range(2)]
-        for t in range(2):
-            round_w1(closing[t][:], 1, t, t + 1, nc.scalar.copy)
-        quantize_w1(closing[0][:], [(1, 0)])
-        quantize_w1(early[2][:], [(0, 2)])
-        late = w1_tile("w1_late", 3, "w1_closing0")
-        round_w1(late[:, 0:2], 1, 2, 4, nc.vector.tensor_copy)
-        round_w1(late[:, 2:3], 0, 3, 4, nc.scalar.copy)
-        quantize_w1(closing[1][:], [(1, 1)])
-        quantize_w1(late[:, 0:1], [(1, 2)])
-        quantize_w1(late[:, 1:3], [(1, 3), (0, 3)])
+        idle = psum.tile([P, BANK], F32, name="idle", tag=f"bank{H_BANKS}")
+        for n in range(2):
+            nc.tensor.matmul_mx(
+                out=idle[:],
+                lhsT=x_words[1, 0][:, :P].bitcast(FP8X4),
+                lhsT_scale=x_scales[1][:, :P],
+                rhs=x_words[0, 0][:].bitcast(FP8X4),
+                rhs_scale=x_scales[0][:, :BANK],
+                start=(n == 0),
+                stop=(n == 1),
+            )
 
         h = [keep.tile([P, S], F32, name=f"h{t}") for t in range(PACK)]
         for t in range(PACK):
@@ -166,7 +198,7 @@ def tile_picked_hop2_gelu_e_kernel(tc, xT, w1, w2, gate, gate2, offs, pos1, pos2
                         lhsT=w1_words[g, t].bitcast(FP8X4),
                         lhsT_scale=w1_scales[g, t],
                         rhs=x_words[g, u][:].bitcast(FP8X4),
-                        rhs_scale=x_scales[g, u][:],
+                        rhs_scale=x_scales[g][:, u * BANK : (u + 1) * BANK],
                         start=(g == 0),
                         stop=(g == PASSES - 1),
                     )
@@ -186,7 +218,7 @@ def tile_picked_hop2_gelu_e_kernel(tc, xT, w1, w2, gate, gate2, offs, pos1, pos2
         def fused_term(t, s, d):
             v0, v1 = V_SLICES[s]
             nc.vector.tensor_tensor(
-                terms[s, d][:, t, :], h[t][:].indirect(entries(pos_sb[d], v0, v1)), gate_sb[:, d, v0:v1], MULT
+                terms[s, d][:, t, :], h[t][:].indirect(entries(pos_sb[d], v0, v1)), gates(d, v0, v1)[:, 0, :], MULT
             )
 
         def fetch(s, d, t0):
@@ -197,7 +229,7 @@ def tile_picked_hop2_gelu_e_kernel(tc, xT, w1, w2, gate, gate2, offs, pos1, pos2
 
         def weigh(s, d, t0):
             v0, v1 = V_SLICES[s]
-            weights = gate_sb[:, d : d + 1, v0:v1].to_broadcast([P, PACK - t0, v1 - v0])
+            weights = gates(d, v0, v1).to_broadcast([P, PACK - t0, v1 - v0])
             nc.vector.tensor_tensor(terms[s, d][:, t0:, :], fetched[s, d][:], weights, MULT)
 
         def add_terms(s):

@@ -176,18 +176,6 @@ def tile_picked_hop2_gelu_e_kernel(tc, xT, w1, w2, gate, gate2, offs, pos1, pos2
         quantize_w1(upper[:], [(0, 2), (0, 3)], "w1_bf1_0")
         quantize_w1(middle[:], [(1, 1), (1, 2)])
 
-        idle = psum.tile([P, BANK], F32, name="idle", tag=f"bank{H_BANKS}")
-        for n in range(2):
-            nc.tensor.matmul_mx(
-                out=idle[:],
-                lhsT=x_words[1, 0][:, :P].bitcast(FP8X4),
-                lhsT_scale=x_scales[1][:, :P],
-                rhs=x_words[0, 0][:].bitcast(FP8X4),
-                rhs_scale=x_scales[0][:, :BANK],
-                start=(n == 0),
-                stop=(n == 1),
-            )
-
         h = [keep.tile([P, S], F32, name=f"h{t}") for t in range(PACK)]
         for t in range(PACK):
             for u in range(HALVES):

@@ -1,6 +1,7 @@
 from contextlib import ExitStack
 
 import concourse.mybir as mybir
+from concourse.masks import make_identity
 
 K, T, S, V, H, N, U = 1024, 2048, 1024, 512, 512, 256, 256
 FLOPS = 2 * K * H * S + 2 * H * N * V
@@ -29,10 +30,14 @@ NEIGHBOURS = 2
 
 VECTOR_ENTRIES = 384
 SCALAR_WEAVES = 128
-H_BANKS = 3
-G_BANK0, G_BANKS = 4, 4
-V_SLICES = [(0, 256), (256, 448), (448, 512)]
-V_PIECES = [[(0, 256)], [(0, 128), (128, 192)], [(0, 64)]]
+H_BANKS = 5
+FIRST_WIDTH = 256
+FUSED = 384
+BLOCKS = FUSED // P
+SUM_BANKS = [2, 3, 4]
+TURN_BANKS = [0, 1, 5]
+GROUPS = [(0, 256), (FUSED, V), (256, FUSED)]
+G_BANKS = [[6, 7], [1, 5], [2, 3]]
 
 
 def interleave_views(dst, src):
@@ -78,13 +83,9 @@ def tile_picked_hop2_gelu_e_kernel(tc, xT, w1, w2, gate, gate2, offs, pos1, pos2
             nc.sync.dma_start(w2_raw[:, t, :], w2.rearrange("(a t r) n -> t a r n", t=PACK, r=RUN)[t])
         pos_sb = [load_list("pos1_sb", pos1), load_list("pos2_sb", pos2)]
         gate_sb = []
-        for v0, v1 in ((0, V // 2), (V // 2, V)):
+        for v0, v1 in ((0, FUSED), (FUSED, V)):
             gate_sb.append(keep.tile([P, NEIGHBOURS, v1 - v0], F32, name=f"gate_sb{v0}"))
             nc.sync.dma_start(gate_sb[-1][:], gate[:, :, v0:v1].rearrange("d p v -> p d v"))
-
-        def gates(d, v0, v1):
-            half = v0 // (V // 2)
-            return gate_sb[half][:, d : d + 1, v0 - half * (V // 2) : v1 - half * (V // 2)]
         gate2_sb = keep.tile([P, NEIGHBOURS, U], F32, name="gate2_sb")
         nc.sync.dma_start(gate2_sb[:], gate2.rearrange("d p v -> p d v"))
         nxt_sb = [load_list("nxt1_sb", nxt1), load_list("nxt2_sb", nxt2)]
@@ -158,8 +159,7 @@ def tile_picked_hop2_gelu_e_kernel(tc, xT, w1, w2, gate, gate2, offs, pos1, pos2
         upper = w1_tile("w1_upper", 2)
         middle = w1_tile("w1_middle", 2)
         words_tile(1, 0, f"x_plane{PASSES - 1}_{PACK - 1}")
-        quantize_x(1, ranges[1][0], 0, P)
-        quantize_x(1, ranges[1][0], P, BANK)
+        quantize_x(1, ranges[1][0], 0, BANK)
         round_w1(w00[:], w1_parts[:, 0, 0:1], nc.scalar.copy)
         round_w1(w01[:], w1_parts[:, 0, 1:2], nc.scalar.copy)
         round_w1(upper[:], w1_parts[:, 0, 2:4], nc.scalar.copy)
@@ -177,98 +177,153 @@ def tile_picked_hop2_gelu_e_kernel(tc, xT, w1, w2, gate, gate2, offs, pos1, pos2
         quantize_w1(middle[:], [(1, 1), (1, 2)])
 
         h = [keep.tile([P, S], F32, name=f"h{t}") for t in range(PACK)]
-        for t in range(PACK):
-            for u in range(HALVES):
-                acc = psum.tile([P, BANK], F32, name=f"acc{t}_{u}", tag=f"bank{(HALVES * t + u) % H_BANKS}")
-                for g in range(PASSES):
-                    nc.tensor.matmul_mx(
-                        out=acc[:],
-                        lhsT=w1_words[g, t].bitcast(FP8X4),
-                        lhsT_scale=w1_scales[g, t],
-                        rhs=x_words[g, u][:].bitcast(FP8X4),
-                        rhs_scale=x_scales[g][:, u * BANK : (u + 1) * BANK],
-                        start=(g == 0),
-                        stop=(g == PASSES - 1),
-                    )
-                nc.scalar.activation(h[t][:, u * BANK : (u + 1) * BANK], acc[:], ACT.Gelu_apprx_tanh)
+        groups = [(0, e, e + FIRST_WIDTH) for e in range(0, S, FIRST_WIDTH)]
+        groups.extend((t, e, e + BANK) for t in range(1, PACK) for e in range(0, S, BANK))
+        for n, (t, e0, e1) in enumerate(groups):
+            acc = psum.tile([P, e1 - e0], F32, name=f"acc{n}", tag=f"bank{n % H_BANKS}")
+            u = e0 // BANK
+            for g in range(PASSES):
+                nc.tensor.matmul_mx(
+                    out=acc[:],
+                    lhsT=w1_words[g, t].bitcast(FP8X4),
+                    lhsT_scale=w1_scales[g, t],
+                    rhs=x_words[g, u][:, e0 - u * BANK : e1 - u * BANK].bitcast(FP8X4),
+                    rhs_scale=x_scales[g][:, e0:e1],
+                    start=(g == 0),
+                    stop=(g == PASSES - 1),
+                )
+            nc.scalar.activation(h[t][:, e0:e1], acc[:], ACT.Gelu_apprx_tanh)
 
-        w2_bf = keep.tile([P, N, PACK], BF16, name="w2_bf", align_bytes=64)
-        dst, src = interleave_views(w2_bf[:], w2_raw[:])
-        nc.vector.tensor_copy(dst, src)
+        w2_halves = [keep.tile([P, P, PACK], BF16, name=f"w2_bf{b}", align_bytes=64) for b in range(G_TILES)]
+        for b in range(G_TILES):
+            nc.vector.tensor_copy(*interleave_views(w2_halves[b][:], w2_raw[:, :, b * P : (b + 1) * P]))
         w2_words = keep.tile([P, N], U32, name="w2_words", align_bytes=64)
         w2_scales = keep.tile([P, N], U8, name="w2_scales", align_bytes=64)
 
-        terms, fetched, z_bf = {}, {}, {}
-        for s, (v0, v1) in enumerate(V_SLICES):
-            for d in range(NEIGHBOURS):
-                terms[s, d] = keep.tile([P, PACK, v1 - v0], F32, name=f"terms{s}_{d}")
+        ident = keep.tile([P, P], F32, name="ident")
+        make_identity(nc, ident[:])
+        for b in range(G_TILES):
+            cols = slice(b * P, (b + 1) * P)
+            quantize(w2_words[:, cols], w2_scales[:, cols], w2_halves[b][:].rearrange("p c t -> p (c t)"))
 
-        def fused_term(t, s, d):
-            v0, v1 = V_SLICES[s]
-            nc.vector.tensor_tensor(
-                terms[s, d][:, t, :], h[t][:].indirect(entries(pos_sb[d], v0, v1)), gates(d, v0, v1)[:, 0, :], MULT
+        terms = {}
+
+        def fused_term(t, d, v0, v1):
+            tile = keep.tile([P, v1 - v0], F32, name=f"terms{t}_{d}_{v0}")
+            nc.vector.tensor_tensor(tile[:], h[t][:].indirect(entries(pos_sb[d], v0, v1)), gate_sb[0][:, d, v0:v1], MULT)
+            for c in range(v0 // P, v1 // P):
+                terms[t, d, c] = tile[:, c * P - v0 : (c + 1) * P - v0]
+
+        sums = {}
+
+        def add_turned(t, c):
+            if c not in sums:
+                sums[c] = psum.tile([P, PACK, P], F32, name=f"sums{c}", tag=f"bank{SUM_BANKS[c]}")
+            for d in range(NEIGHBOURS):
+                nc.tensor.matmul(sums[c][:, t, :], terms[t, d, c], ident[:], is_transpose=True, start=(d == 0), stop=(d == 1))
+
+        z_bf = [keep.tile([P, v1 - v0, PACK], BF16, name=f"z_bf{n}", align_bytes=64) for n, (v0, v1) in enumerate(GROUPS)]
+        rounded, turned = {}, {}
+
+        def round_sums(c):
+            rounded[c] = keep.tile([P, 2, P, 2], BF16, name=f"rounded{c}", tag=f"rounded{c}", align_bytes=64)
+            nc.scalar.copy(
+                rounded[c][:].rearrange("v u (q i) e -> v u q e i", i=2),
+                sums[c][:].rearrange("v (u e) (q i) -> v u q e i", e=2, i=2),
+            )
+            turned[c] = psum.tile([P, 2, P], F32, name=f"turned{c}", tag=f"bank{TURN_BANKS[c]}")
+            words = rounded[c][:].rearrange("v u p e -> v (u p e)").bitcast(F32)
+            for u in range(2):
+                nc.tensor.transpose(turned[c][:, u, :], words[:, u * P : (u + 1) * P], ident[:])
+
+        def lay_words(c):
+            n = 0 if c < 2 else 2
+            c0 = c * P - GROUPS[n][0]
+            words = z_bf[n][:, c0 : c0 + P, :].rearrange("p v t -> p (v t)").bitcast(F32)
+            nc.scalar.copy(
+                words.rearrange("p (q i u) -> p q u i", i=2, u=2), turned[c][:].rearrange("p u (q i) -> p q u i", i=2)
             )
 
-        def fetch(s, d, t0):
-            v0, v1 = V_SLICES[s]
-            fetched[s, d] = keep.tile([P, PACK - t0, v1 - v0], F32, name=f"fetched{s}_{d}")
-            for t in range(t0, PACK):
-                nc.scalar.activation(fetched[s, d][:, t - t0, :], h[t][:].indirect(entries(pos_sb[d], v0, v1)), ACT.Copy)
+        rest = V - FUSED
+        fetched = [keep.tile([P, PACK, rest], F32, name=f"fetched{d}") for d in range(NEIGHBOURS)]
+        weighed = {}
 
-        def weigh(s, d, t0):
-            v0, v1 = V_SLICES[s]
-            weights = gates(d, v0, v1).to_broadcast([P, PACK - t0, v1 - v0])
-            nc.vector.tensor_tensor(terms[s, d][:, t0:, :], fetched[s, d][:], weights, MULT)
+        def fetch(d):
+            for t in range(PACK):
+                nc.scalar.activation(fetched[d][:, t, :], h[t][:].indirect(entries(pos_sb[d], FUSED, V)), ACT.Copy)
 
-        def add_terms(s):
-            v0, v1 = V_SLICES[s]
-            z_bf[s] = keep.tile([P, v1 - v0, PACK], BF16, name=f"z_bf{s}", align_bytes=64)
-            first, second = [terms[s, d][:].rearrange("p t (c i) -> p c t i", i=2) for d in range(NEIGHBOURS)]
-            nc.vector.tensor_tensor(z_bf[s][:].rearrange("p (c i) t -> p c t i", i=2), first, second, ADD)
+        def weigh(d, c0, c1):
+            weights = gate_sb[1][:, d : d + 1, c0:c1].to_broadcast([P, PACK, c1 - c0])
+            weighed[d, c0] = keep.tile([P, PACK, c1 - c0], F32, name=f"weighed{d}_{c0}")
+            nc.vector.tensor_tensor(weighed[d, c0][:], fetched[d][:, :, c0:c1], weights, MULT)
+
+        def add_rest(c0, c1):
+            first = weighed[0, 0][:, :, c0:c1].rearrange("p t (c i) -> p c t i", i=2)
+            second = weighed[1, c0][:].rearrange("p t (c i) -> p c t i", i=2)
+            nc.vector.tensor_tensor(z_bf[1][:, c0:c1, :].rearrange("p (c i) t -> p c t i", i=2), first, second, ADD)
 
         g_sb = [keep.tile([P, V], F32, name=f"g{b}") for b in range(G_TILES)]
 
-        def second_product(s):
-            v0, v1 = V_SLICES[s]
-            words = keep.tile([P, v1 - v0], U32, name=f"z_words{s}", align_bytes=64)
-            scales = keep.tile([P, v1 - v0], U8, name=f"z_scales{s}", align_bytes=64)
-            for c0, c1 in V_PIECES[s]:
-                quantize(words[:, c0:c1], scales[:, c0:c1], z_bf[s][:, c0:c1, :].rearrange("p c t -> p (c t)"))
-            for b in range(G_TILES):
-                tag = f"bank{G_BANK0 + (G_TILES * s + b) % G_BANKS}"
-                bank = psum.tile([P, v1 - v0], F32, name=f"g_acc{s}_{b}", tag=tag)
-                for c0, c1 in V_PIECES[s]:
-                    nc.tensor.matmul_mx(
-                        out=bank[:, c0:c1],
-                        lhsT=w2_words[:, b * P : (b + 1) * P].bitcast(FP8X4),
-                        lhsT_scale=w2_scales[:, b * P : (b + 1) * P],
-                        rhs=words[:, c0:c1].bitcast(FP8X4),
-                        rhs_scale=scales[:, c0:c1],
-                        start=True,
-                        stop=True,
-                    )
-                nc.scalar.activation(g_sb[b][:, v0:v1], bank[:], ACT.Relu)
+        z_codes = {}
 
-        quantize(w2_words[:], w2_scales[:], w2_bf[:].rearrange("p c t -> p (c t)"))
-        for t in range(PACK):
+        def quantize_z(n, tag=None):
+            v0, v1 = GROUPS[n]
+            words = keep.tile([P, v1 - v0], U32, name=f"z_words{n}", tag=tag or f"z_words{n}", align_bytes=64)
+            scales = keep.tile([P, v1 - v0], U8, name=f"z_scales{n}", align_bytes=64)
+            quantize(words[:], scales[:], z_bf[n][:].rearrange("p c t -> p (c t)"))
+            z_codes[n] = (words, scales)
+
+        def second_product(n, last=False):
+            v0, v1 = GROUPS[n]
+            words, scales = z_codes[n]
+            for b in range(G_TILES):
+                bank = psum.tile([P, v1 - v0], F32, name=f"g_acc{n}_{b}", tag=f"bank{G_BANKS[n][b]}")
+                nc.tensor.matmul_mx(
+                    out=bank[:],
+                    lhsT=w2_words[:, b * P : (b + 1) * P].bitcast(FP8X4),
+                    lhsT_scale=w2_scales[:, b * P : (b + 1) * P],
+                    rhs=words[:].bitcast(FP8X4),
+                    rhs_scale=scales[:],
+                    start=True,
+                    stop=True,
+                )
+                if last and b == 1:
+                    nc.vector.tensor_scalar_max(g_sb[b][:, v0:v1], bank[:], 0.0)
+                else:
+                    nc.scalar.activation(g_sb[b][:, v0:v1], bank[:], ACT.Relu)
+
+        last = BLOCKS - 1
+        for t in range(PACK - 1):
             for d in range(NEIGHBOURS):
-                fused_term(t, 0, d)
-            if t == 0:
-                fused_term(0, 1, 0)
-        fetch(1, 0, 1)
-        fetch(1, 1, 0)
-        fetch(2, 0, 0)
-        fetch(2, 1, 0)
-        weigh(1, 0, 1)
-        add_terms(0)
-        weigh(1, 1, 0)
-        second_product(0)
-        add_terms(1)
-        weigh(2, 0, 0)
-        weigh(2, 1, 0)
-        second_product(1)
-        add_terms(2)
-        second_product(2)
+                fused_term(t, d, 0, last * P if (t, d) == (0, 1) else FUSED)
+        extra = keep.tile([P, P], F32, name="extra")
+        extra_terms = keep.tile([P, P], F32, name="extra_terms")
+        nc.scalar.activation(extra[:], h[0][:].indirect(entries(pos_sb[1], last * P, FUSED)), ACT.Copy)
+        terms[0, 1, last] = extra_terms[:]
+        nc.vector.tensor_tensor(extra_terms[:], extra[:], gate_sb[0][:, 1, last * P :], MULT)
+        for c in range(BLOCKS):
+            for d in range(NEIGHBOURS):
+                fused_term(PACK - 1, d, c * P, (c + 1) * P)
+        for c in range(BLOCKS):
+            for t in range(PACK - 1) if c < last else (1, 2, 0):
+                add_turned(t, c)
+        fetch(0)
+        fetch(1)
+        for c in range(BLOCKS):
+            add_turned(PACK - 1, c)
+            round_sums(c)
+        for c in range(BLOCKS):
+            lay_words(c)
+        weigh(0, 0, rest)
+        for c0 in (0, rest // 2):
+            weigh(1, c0, c0 + rest // 2)
+        for c0 in (0, rest // 2):
+            add_rest(c0, c0 + rest // 2)
+        quantize_z(1)
+        quantize_z(0, "rounded2")
+        quantize_z(2)
+        for n in (1, 0, 2):
+            second_product(n, last=True)
 
         pair = [keep.tile([P, NEIGHBOURS, U], F32, name=f"pair{b}") for b in range(G_TILES)]
         result = [keep.tile([P, U], F32, name=f"result{b}") for b in range(G_TILES)]

@@ -295,12 +295,13 @@ def tile_picked_hop2_gelu_e_kernel(tc, xT, w1, w2, gate, gate2, offs, pos1, pos2
         last = BLOCKS - 1
         for t in range(PACK - 1):
             for d in range(NEIGHBOURS):
-                fused_term(t, d, 0, last * P if (t, d) == (0, 1) else FUSED)
-        extra = keep.tile([P, P], F32, name="extra")
-        extra_terms = keep.tile([P, P], F32, name="extra_terms")
-        nc.scalar.activation(extra[:], h[0][:].indirect(entries(pos_sb[1], last * P, FUSED)), ACT.Copy)
-        terms[0, 1, last] = extra_terms[:]
-        nc.vector.tensor_tensor(extra_terms[:], extra[:], gate_sb[0][:, 1, last * P :], MULT)
+                fused_term(t, d, 0, last * P if t == 0 else FUSED)
+        extra = keep.tile([P, NEIGHBOURS, P], F32, name="extra")
+        extra_terms = keep.tile([P, NEIGHBOURS, P], F32, name="extra_terms")
+        for d in range(NEIGHBOURS):
+            nc.scalar.activation(extra[:, d], h[0][:].indirect(entries(pos_sb[d], last * P, FUSED)), ACT.Copy)
+            terms[0, d, last] = extra_terms[:, d]
+        nc.vector.tensor_tensor(extra_terms[:], extra[:], gate_sb[0][:, :, last * P :], MULT)
         for c in range(BLOCKS):
             for d in range(NEIGHBOURS):
                 fused_term(PACK - 1, d, c * P, (c + 1) * P)

@@ -34,6 +34,7 @@ H_BANKS = 5
 FIRST_WIDTH = 256
 FUSED = 384
 BLOCKS = FUSED // P
+EXTRA = 128
 SUM_BANKS = [2, 3, 4]
 TURN_BANKS = [0, 1, 5]
 GROUPS = [(0, 256), (FUSED, V), (256, FUSED)]
@@ -245,17 +246,17 @@ def tile_picked_hop2_gelu_e_kernel(tc, xT, w1, w2, gate, gate2, offs, pos1, pos2
             )
 
         rest = V - FUSED
-        fetched = [keep.tile([P, PACK, rest], F32, name=f"fetched{d}") for d in range(NEIGHBOURS)]
+        fetched = keep.tile([P, NEIGHBOURS, PACK, EXTRA + rest], F32, name="fetched")
         weighed = {}
 
-        def fetch(d):
-            for t in range(PACK):
-                nc.scalar.activation(fetched[d][:, t, :], h[t][:].indirect(entries(pos_sb[d], FUSED, V)), ACT.Copy)
+        def fetch(t, d, extra=0):
+            window = h[t][:].indirect(entries(pos_sb[d], FUSED - extra, V))
+            nc.scalar.activation(fetched[:, d, t, EXTRA - extra :], window, ACT.Copy)
 
         def weigh(d, c0, c1):
             weights = gate_sb[1][:, d : d + 1, c0:c1].to_broadcast([P, PACK, c1 - c0])
             weighed[d, c0] = keep.tile([P, PACK, c1 - c0], F32, name=f"weighed{d}_{c0}")
-            nc.vector.tensor_tensor(weighed[d, c0][:], fetched[d][:, :, c0:c1], weights, MULT)
+            nc.vector.tensor_tensor(weighed[d, c0][:], fetched[:, d, :, EXTRA + c0 : EXTRA + c1], weights, MULT)
 
         def add_rest(c0, c1):
             first = weighed[0, 0][:, :, c0:c1].rearrange("p t (c i) -> p c t i", i=2)
@@ -266,51 +267,63 @@ def tile_picked_hop2_gelu_e_kernel(tc, xT, w1, w2, gate, gate2, offs, pos1, pos2
 
         z_codes = {}
 
-        def quantize_z(n, tag=None):
-            v0, v1 = GROUPS[n]
-            words = keep.tile([P, v1 - v0], U32, name=f"z_words{n}", tag=tag or f"z_words{n}", align_bytes=64)
-            scales = keep.tile([P, v1 - v0], U8, name=f"z_scales{n}", align_bytes=64)
-            quantize(words[:], scales[:], z_bf[n][:].rearrange("p c t -> p (c t)"))
-            z_codes[n] = (words, scales)
+        def quantize_z(n, c0, c1, tag=None):
+            if n not in z_codes:
+                v0, v1 = GROUPS[n]
+                words = keep.tile([P, v1 - v0], U32, name=f"z_words{n}", tag=tag or f"z_words{n}", align_bytes=64)
+                scales = keep.tile([P, v1 - v0], U8, name=f"z_scales{n}", align_bytes=64)
+                z_codes[n] = (words, scales)
+            words, scales = z_codes[n]
+            quantize(words[:, c0:c1], scales[:, c0:c1], z_bf[n][:, c0:c1].rearrange("p c t -> p (c t)"))
 
         def second_product(n, last=False):
             v0, v1 = GROUPS[n]
             words, scales = z_codes[n]
             for b in range(G_TILES):
                 bank = psum.tile([P, v1 - v0], F32, name=f"g_acc{n}_{b}", tag=f"bank{G_BANKS[n][b]}")
-                nc.tensor.matmul_mx(
-                    out=bank[:],
-                    lhsT=w2_words[:, b * P : (b + 1) * P].bitcast(FP8X4),
-                    lhsT_scale=w2_scales[:, b * P : (b + 1) * P],
-                    rhs=words[:].bitcast(FP8X4),
-                    rhs_scale=scales[:],
-                    start=True,
-                    stop=True,
-                )
-                if last and b == 1:
+                for c0 in range(0, v1 - v0, P):
+                    nc.tensor.matmul_mx(
+                        out=bank[:, c0 : c0 + P],
+                        lhsT=w2_words[:, b * P : (b + 1) * P].bitcast(FP8X4),
+                        lhsT_scale=w2_scales[:, b * P : (b + 1) * P],
+                        rhs=words[:, c0 : c0 + P].bitcast(FP8X4),
+                        rhs_scale=scales[:, c0 : c0 + P],
+                        start=True,
+                        stop=True,
+                    )
+                if b == 1 and not last:
                     nc.vector.tensor_scalar_max(g_sb[b][:, v0:v1], bank[:], 0.0)
                 else:
                     nc.scalar.activation(g_sb[b][:, v0:v1], bank[:], ACT.Relu)
 
         last = BLOCKS - 1
+        cut = FUSED - EXTRA
+        shared = keep.tile([P, NEIGHBOURS, FUSED], F32, name="shared_terms")
         for t in range(PACK - 1):
             for d in range(NEIGHBOURS):
-                fused_term(t, d, 0, last * P if t == 0 else FUSED)
-        extra = keep.tile([P, NEIGHBOURS, P], F32, name="extra")
-        extra_terms = keep.tile([P, NEIGHBOURS, P], F32, name="extra_terms")
+                if t == 1:
+                    window = h[t][:].indirect(entries(pos_sb[d], 0, cut))
+                    nc.vector.tensor_tensor(shared[:, d, :cut], window, gate_sb[0][:, d, :cut], MULT)
+                    for c in range(BLOCKS):
+                        terms[t, d, c] = shared[:, d, c * P : (c + 1) * P]
+                else:
+                    fused_term(t, d, 0, FUSED)
         for d in range(NEIGHBOURS):
-            nc.scalar.activation(extra[:, d], h[0][:].indirect(entries(pos_sb[d], last * P, FUSED)), ACT.Copy)
-            terms[0, d, last] = extra_terms[:, d]
-        nc.vector.tensor_tensor(extra_terms[:], extra[:], gate_sb[0][:, :, last * P :], MULT)
+            fetch(1, d, EXTRA)
         for c in range(BLOCKS):
             for d in range(NEIGHBOURS):
                 fused_term(PACK - 1, d, c * P, (c + 1) * P)
+            if c == last - 1:
+                nc.vector.tensor_tensor(shared[:, :, cut:], fetched[:, :, 1, :EXTRA], gate_sb[0][:, :, cut:], MULT)
         for c in range(BLOCKS):
-            for t in range(PACK - 1) if c < last else (1, 2, 0):
+            for t in range(PACK - 1) if c < last else (0, 2):
                 add_turned(t, c)
-        fetch(0)
-        fetch(1)
+        for d in range(NEIGHBOURS):
+            for t in (0, 2, 3):
+                fetch(t, d)
         for c in range(BLOCKS):
+            if c == last:
+                add_turned(1, c)
             add_turned(PACK - 1, c)
             round_sums(c)
         for c in range(BLOCKS):
@@ -320,11 +333,12 @@ def tile_picked_hop2_gelu_e_kernel(tc, xT, w1, w2, gate, gate2, offs, pos1, pos2
             weigh(1, c0, c0 + rest // 2)
         for c0 in (0, rest // 2):
             add_rest(c0, c0 + rest // 2)
-        quantize_z(1)
-        quantize_z(0, "rounded2")
-        quantize_z(2)
+        quantize_z(0, 0, P)
+        quantize_z(1, 0, P)
+        quantize_z(0, P, 2 * P)
+        quantize_z(2, 0, P)
         for n in (1, 0, 2):
-            second_product(n, last=True)
+            second_product(n, last=(n == 2))
 
         pair = [keep.tile([P, NEIGHBOURS, U], F32, name=f"pair{b}") for b in range(G_TILES)]
         result = [keep.tile([P, U], F32, name=f"result{b}") for b in range(G_TILES)]

from contextlib import ExitStack

import concourse.mybir as mybir
from concourse.masks import make_identity

K, T, S, V, H, N, U = 1024, 2048, 1024, 512, 512, 256, 256
FLOPS = 2 * K * H * S + 2 * H * N * V

F32 = mybir.dt.float32
BF16 = mybir.dt.bfloat16
U32 = mybir.dt.uint32
U16 = mybir.dt.uint16
U8 = mybir.dt.uint8
FP8X4 = mybir.dt.float8_e4m3fn_x4
ACT = mybir.ActivationFunctionType
MULT = mybir.AluOpType.mult
ADD = mybir.AluOpType.add

P = 128
PACK = 4
RUN = 4
LIST_ROWS = 16
K_PASS = P * PACK
PASSES = K // K_PASS
BANK = 512
HALVES = S // BANK
PAIRS = PASSES * PACK // 2
G_TILES = N // P
NEIGHBOURS = 2

VECTOR_ENTRIES = 384
SCALAR_WEAVES = 128
H_BANKS = 5
FIRST_WIDTH = 256
FUSED = 384
BLOCKS = FUSED // P
EXTRA = 128
SUM_BANKS = [2, 3, 4]
TURN_BANKS = [0, 1, 5]
GROUPS = [(0, 256), (FUSED, V), (256, FUSED)]
G_BANKS = [[6, 7], [1, 5], [2, 3]]


def interleave_views(dst, src):
    return (dst.rearrange("p (c i) j -> p c j i", i=4), src.rearrange("p j (c i) -> p c j i", i=4))


def entries(offsets, e0, e1):
    return offsets[:, e0 // LIST_ROWS : e1 // LIST_ROWS]


def tile_picked_hop2_gelu_e_kernel(tc, xT, w1, w2, gate, gate2, offs, pos1, pos2, nxt1, nxt2, out):
    nc = tc.nc
    with ExitStack() as ctx:
        keep = ctx.enter_context(tc.tile_pool(name="keep", bufs=1))
        psum = ctx.enter_context(tc.psum_pool(name="psum", bufs=1))

        def load_list(name, src):
            tile = keep.tile(list(src.shape), U16, name=name)
            nc.sync.dma_start(tile[:], src)
            return tile

        def load_plane(g, j):
            tile = keep.tile([P, T], F32, name=f"x_plane{g}_{j}", tag=f"x_plane{g}_{j}", align_bytes=64)
            nc.sync.dma_start(tile[:], xT[g * K_PASS : (g + 1) * K_PASS, :].rearrange("(p j) c -> j p c", j=PACK)[j])
            return tile

        def quantize(words, scales, values):
            nc.vector.quantize_mx(out=words.bitcast(FP8X4), scales=scales, in_=values)

        warm = keep.tile([P, 2], F32, name="warm")
        nc.vector.memset(warm[:, 0:1], 0.0)
        nc.scalar.activation(warm[:, 1:2], warm[:, 0:1], ACT.Gelu_apprx_tanh)

        planes = {(0, 0): load_plane(0, 0)}
        offs_sb = load_list("offs_sb", offs)
        for n in range(1, PASSES * PACK):
            planes[n // PACK, n % PACK] = load_plane(n // PACK, n % PACK)
        w1_raw = keep.tile([P, PASSES, PACK, H], F32, name="w1_raw")
        for g in range(PASSES):
            nc.sync.dma_start(w1_raw[:, g], w1[g * K_PASS : (g + 1) * K_PASS, :].rearrange("(p j) c -> p j c", j=PACK))
        w2_raw = keep.tile([P, PACK, N], F32, name="w2_raw")
        for t in range(PACK):
            nc.sync.dma_start(w2_raw[:, t, :], w2.rearrange("(a t r) n -> t a r n", t=PACK, r=RUN)[t])
        pos_sb = [load_list("pos1_sb", pos1), load_list("pos2_sb", pos2)]
        gate_sb = []
        for v0, v1 in ((0, FUSED), (FUSED, V)):
            gate_sb.append(keep.tile([P, NEIGHBOURS, v1 - v0], F32, name=f"gate_sb{v0}"))
            nc.sync.dma_start(gate_sb[-1][:], gate[:, :, v0:v1].rearrange("d p v -> p d v"))
        gate2_sb = keep.tile([P, NEIGHBOURS, U], F32, name="gate2_sb")
        nc.sync.dma_start(gate2_sb[:], gate2.rearrange("d p v -> p d v"))
        nxt_sb = [load_list("nxt1_sb", nxt1), load_list("nxt2_sb", nxt2)]

        ranges = [[(0, BANK), (BANK, S)], [(0, BANK), (BANK, BANK + SCALAR_WEAVES), (BANK + SCALAR_WEAVES, S)]]
        x_bf = [
            {r: keep.tile([P, r[1] - r[0], PACK], BF16, name=f"x_bf{g}_{r[0]}", align_bytes=64) for r in ranges[g]}
            for g in range(PASSES)
        ]
        x_words = {}
        x_scales = [keep.tile([P, S], U8, name=f"x_scales{g}", align_bytes=64) for g in range(PASSES)]
        picked = [keep.tile([P, 2, S - VECTOR_ENTRIES], F32, name=f"picked{n}") for n in range(PAIRS)]

        def gather_plane(g, j, cut):
            window = planes[g, j][:]
            nc.vector.tensor_copy(x_bf[g][0, BANK][:, :cut, j], window.indirect(entries(offs_sb, 0, cut)))
            fetched_part = picked[2 * g + j // 2][:, j % 2, cut - VECTOR_ENTRIES :]
            nc.scalar.activation(fetched_part, window.indirect(entries(offs_sb, cut, S)), ACT.Copy)

        def interleave_x(n, r, rows, copy):
            g, j0 = n // 2, 2 * (n % 2)
            e0 = max(r[0], VECTOR_ENTRIES)
            source = picked[n][:, :rows, e0 - VECTOR_ENTRIES : r[1] - VECTOR_ENTRIES]
            copy(*interleave_views(x_bf[g][r][:, e0 - r[0] :, j0 : j0 + rows], source))

        def quantize_x(g, r, e0, e1):
            values = x_bf[g][r][:, e0 - r[0] : e1 - r[0], :].rearrange("p c j -> p (c j)")
            u = r[0] // BANK
            quantize(x_words[g, u][:, e0 - u * BANK : e1 - u * BANK], x_scales[g][:, e0:e1], values)

        def words_tile(g, u, tag):
            x_words[g, u] = keep.tile([P, BANK], U32, name=f"x_words{g}_{u}", tag=tag, align_bytes=64)

        for n in range(PAIRS - 1):
            g = n // 2
            for e in range(2):
                gather_plane(g, 2 * (n % 2) + e, VECTOR_ENTRIES)
                if n == 2:
                    words_tile(0, e, f"x_words0_{e}")
                    quantize_x(0, ranges[0][e], *ranges[0][e])
            for r in ranges[g][1:]:
                interleave_x(n, r, 2, nc.vector.tensor_copy)
            interleave_x(n, ranges[g][0], 2, nc.scalar.copy)
        gather_plane(1, 2, VECTOR_ENTRIES)
        interleave_x(PAIRS - 1, ranges[1][0], 1, nc.vector.tensor_copy)
        gather_plane(1, 3, BANK)
        interleave_x(PAIRS - 1, ranges[1][1], 2, nc.scalar.copy)
        interleave_x(PAIRS - 1, ranges[1][2], 2, nc.vector.tensor_copy)

        w1_words, w1_scales = {}, {}

        def w1_tile(name, count):
            return keep.tile([P, count, P, PACK], BF16, name=name, tag=name, align_bytes=64)

        w1_parts = w1_raw[:].rearrange("p g j (a t r) -> p g t a j r", t=PACK, r=RUN)

        def round_w1(grouped, parts, copy):
            copy(grouped.rearrange("p n (a r) j -> p n a j r", r=RUN), parts)

        def quantize_w1(grouped, parts, tag=None):
            g, t = parts[0]
            name = f"w1_words{g}_{t}"
            words = keep.tile([P, len(parts) * P], U32, name=name, tag=tag or name, align_bytes=64)
            scales = keep.tile([P, len(parts) * P], U8, name=f"w1_scales{g}_{t}", align_bytes=64)
            quantize(words[:], scales[:], grouped.rearrange("p t m j -> p (t m j)"))
            for n, part in enumerate(parts):
                w1_words[part] = words[:, n * P : (n + 1) * P]
                w1_scales[part] = scales[:, n * P : (n + 1) * P]

        w00, w01, w10, w13 = [w1_tile(f"w1_bf{g}_{t}", 1) for g, t in ((0, 0), (0, 1), (1, 0), (1, 3))]
        upper = w1_tile("w1_upper", 2)
        middle = w1_tile("w1_middle", 2)
        words_tile(1, 0, f"x_plane{PASSES - 1}_{PACK - 1}")
        quantize_x(1, ranges[1][0], 0, BANK)
        round_w1(w00[:], w1_parts[:, 0, 0:1], nc.scalar.copy)
        round_w1(w01[:], w1_parts[:, 0, 1:2], nc.scalar.copy)
        round_w1(upper[:], w1_parts[:, 0, 2:4], nc.scalar.copy)
        quantize_w1(w00[:], [(0, 0)])
        words_tile(1, 1, "w1_bf0_0")
        for r in ranges[1][1:]:
            quantize_x(1, r, *r)
        quantize_w1(w01[:], [(0, 1)])
        round_w1(w10[:], w1_parts[:, 1, 0:1], nc.vector.tensor_copy)
        round_w1(w13[:], w1_parts[:, 1, 3:4], nc.vector.tensor_copy)
        round_w1(middle[:], w1_parts[:, 1, 1:3], nc.scalar.copy)
        quantize_w1(w10[:], [(1, 0)])
        quantize_w1(w13[:], [(1, 3)])
        quantize_w1(upper[:], [(0, 2), (0, 3)], "w1_bf1_0")
        quantize_w1(middle[:], [(1, 1), (1, 2)])

        h = [keep.tile([P, S], F32, name=f"h{t}") for t in range(PACK)]
        groups = [(0, e, e + FIRST_WIDTH) for e in range(0, S, FIRST_WIDTH)]
        groups.extend((t, e, e + BANK) for t in range(1, PACK) for e in range(0, S, BANK))
        for n, (t, e0, e1) in enumerate(groups):
            acc = psum.tile([P, e1 - e0], F32, name=f"acc{n}", tag=f"bank{n % H_BANKS}")
            u = e0 // BANK
            for g in range(PASSES):
                nc.tensor.matmul_mx(
                    out=acc[:],
                    lhsT=w1_words[g, t].bitcast(FP8X4),
                    lhsT_scale=w1_scales[g, t],
                    rhs=x_words[g, u][:, e0 - u * BANK : e1 - u * BANK].bitcast(FP8X4),
                    rhs_scale=x_scales[g][:, e0:e1],
                    start=(g == 0),
                    stop=(g == PASSES - 1),
                )
            nc.scalar.activation(h[t][:, e0:e1], acc[:], ACT.Gelu_apprx_tanh)

        w2_halves = [keep.tile([P, P, PACK], BF16, name=f"w2_bf{b}", align_bytes=64) for b in range(G_TILES)]
        for b in range(G_TILES):
            nc.vector.tensor_copy(*interleave_views(w2_halves[b][:], w2_raw[:, :, b * P : (b + 1) * P]))
        w2_words = keep.tile([P, N], U32, name="w2_words", align_bytes=64)
        w2_scales = keep.tile([P, N], U8, name="w2_scales", align_bytes=64)

        ident = keep.tile([P, P], F32, name="ident")
        make_identity(nc, ident[:])
        for b in range(G_TILES):
            cols = slice(b * P, (b + 1) * P)
            quantize(w2_words[:, cols], w2_scales[:, cols], w2_halves[b][:].rearrange("p c t -> p (c t)"))

        terms = {}

        def fused_term(t, d, v0, v1):
            tile = keep.tile([P, v1 - v0], F32, name=f"terms{t}_{d}_{v0}")
            nc.vector.tensor_tensor(tile[:], h[t][:].indirect(entries(pos_sb[d], v0, v1)), gate_sb[0][:, d, v0:v1], MULT)
            for c in range(v0 // P, v1 // P):
                terms[t, d, c] = tile[:, c * P - v0 : (c + 1) * P - v0]

        sums = {}

        def add_turned(t, c):
            if c not in sums:
                sums[c] = psum.tile([P, PACK, P], F32, name=f"sums{c}", tag=f"bank{SUM_BANKS[c]}")
            for d in range(NEIGHBOURS):
                nc.tensor.matmul(sums[c][:, t, :], terms[t, d, c], ident[:], is_transpose=True, start=(d == 0), stop=(d == 1))

        z_bf = [keep.tile([P, v1 - v0, PACK], BF16, name=f"z_bf{n}", align_bytes=64) for n, (v0, v1) in enumerate(GROUPS)]
        rounded, turned = {}, {}

        def round_sums(c):
            rounded[c] = keep.tile([P, 2, P, 2], BF16, name=f"rounded{c}", tag=f"rounded{c}", align_bytes=64)
            nc.scalar.copy(
                rounded[c][:].rearrange("v u (q i) e -> v u q e i", i=2),
                sums[c][:].rearrange("v (u e) (q i) -> v u q e i", e=2, i=2),
            )
            turned[c] = psum.tile([P, 2, P], F32, name=f"turned{c}", tag=f"bank{TURN_BANKS[c]}")
            words = rounded[c][:].rearrange("v u p e -> v (u p e)").bitcast(F32)
            for u in range(2):
                nc.tensor.transpose(turned[c][:, u, :], words[:, u * P : (u + 1) * P], ident[:])

        def lay_words(c):
            n = 0 if c < 2 else 2
            c0 = c * P - GROUPS[n][0]
            words = z_bf[n][:, c0 : c0 + P, :].rearrange("p v t -> p (v t)").bitcast(F32)
            nc.scalar.copy(
                words.rearrange("p (q i u) -> p q u i", i=2, u=2), turned[c][:].rearrange("p u (q i) -> p q u i", i=2)
            )

        rest = V - FUSED
        fetched = keep.tile([P, NEIGHBOURS, PACK, EXTRA + rest], F32, name="fetched")
        weighed = {}

        def fetch(t, d, extra=0):
            window = h[t][:].indirect(entries(pos_sb[d], FUSED - extra, V))
            nc.scalar.activation(fetched[:, d, t, EXTRA - extra :], window, ACT.Copy)

        def weigh(d, c0, c1):
            weights = gate_sb[1][:, d : d + 1, c0:c1].to_broadcast([P, PACK, c1 - c0])
            weighed[d, c0] = keep.tile([P, PACK, c1 - c0], F32, name=f"weighed{d}_{c0}")
            nc.vector.tensor_tensor(weighed[d, c0][:], fetched[:, d, :, EXTRA + c0 : EXTRA + c1], weights, MULT)

        def add_rest(c0, c1):
            first = weighed[0, 0][:, :, c0:c1].rearrange("p t (c i) -> p c t i", i=2)
            second = weighed[1, c0][:].rearrange("p t (c i) -> p c t i", i=2)
            nc.vector.tensor_tensor(z_bf[1][:, c0:c1, :].rearrange("p (c i) t -> p c t i", i=2), first, second, ADD)

        g_sb = [keep.tile([P, V], F32, name=f"g{b}") for b in range(G_TILES)]

        z_codes = {}

        def quantize_z(n, c0, c1, tag=None):
            if n not in z_codes:
                v0, v1 = GROUPS[n]
                words = keep.tile([P, v1 - v0], U32, name=f"z_words{n}", tag=tag or f"z_words{n}", align_bytes=64)
                scales = keep.tile([P, v1 - v0], U8, name=f"z_scales{n}", align_bytes=64)
                z_codes[n] = (words, scales)
            words, scales = z_codes[n]
            quantize(words[:, c0:c1], scales[:, c0:c1], z_bf[n][:, c0:c1].rearrange("p c t -> p (c t)"))

        def second_product(n, last=False):
            v0, v1 = GROUPS[n]
            words, scales = z_codes[n]
            for b in range(G_TILES):
                bank = psum.tile([P, v1 - v0], F32, name=f"g_acc{n}_{b}", tag=f"bank{G_BANKS[n][b]}")
                for c0 in range(0, v1 - v0, P):
                    nc.tensor.matmul_mx(
                        out=bank[:, c0 : c0 + P],
                        lhsT=w2_words[:, b * P : (b + 1) * P].bitcast(FP8X4),
                        lhsT_scale=w2_scales[:, b * P : (b + 1) * P],
                        rhs=words[:, c0 : c0 + P].bitcast(FP8X4),
                        rhs_scale=scales[:, c0 : c0 + P],
                        start=True,
                        stop=True,
                    )
                if b == 1 and not last:
                    nc.vector.tensor_scalar_max(g_sb[b][:, v0:v1], bank[:], 0.0)
                else:
                    nc.scalar.activation(g_sb[b][:, v0:v1], bank[:], ACT.Relu)

        last = BLOCKS - 1
        cut = FUSED - EXTRA
        shared = keep.tile([P, NEIGHBOURS, FUSED], F32, name="shared_terms")
        for t in range(PACK - 1):
            for d in range(NEIGHBOURS):
                if t == 1:
                    window = h[t][:].indirect(entries(pos_sb[d], 0, cut))
                    nc.vector.tensor_tensor(shared[:, d, :cut], window, gate_sb[0][:, d, :cut], MULT)
                    for c in range(BLOCKS):
                        terms[t, d, c] = shared[:, d, c * P : (c + 1) * P]
                else:
                    fused_term(t, d, 0, FUSED)
        for d in range(NEIGHBOURS):
            fetch(1, d, EXTRA)
        for c in range(BLOCKS):
            for d in range(NEIGHBOURS):
                fused_term(PACK - 1, d, c * P, (c + 1) * P)
            if c == last - 1:
                nc.vector.tensor_tensor(shared[:, :, cut:], fetched[:, :, 1, :EXTRA], gate_sb[0][:, :, cut:], MULT)
        for c in range(BLOCKS):
            for t in range(PACK - 1) if c < last else (0, 2):
                add_turned(t, c)
        for d in range(NEIGHBOURS):
            for t in (0, 2, 3):
                fetch(t, d)
        for c in range(BLOCKS):
            if c == last:
                add_turned(1, c)
            add_turned(PACK - 1, c)
            round_sums(c)
        for c in range(BLOCKS):
            lay_words(c)
        weigh(0, 0, rest)
        for c0 in (0, rest // 2):
            weigh(1, c0, c0 + rest // 2)
        for c0 in (0, rest // 2):
            add_rest(c0, c0 + rest // 2)
        quantize_z(0, 0, P)
        quantize_z(1, 0, P)
        quantize_z(0, P, 2 * P)
        quantize_z(2, 0, P)
        for n in (1, 0, 2):
            second_product(n, last=(n == 2))

        pair = [keep.tile([P, NEIGHBOURS, U], F32, name=f"pair{b}") for b in range(G_TILES)]
        result = [keep.tile([P, U], F32, name=f"result{b}") for b in range(G_TILES)]
        plain = [keep.tile([P, U], F32, name=f"plain{b}") for b in range(G_TILES)]
        for b in range(G_TILES):
            nc.vector.tensor_tensor(pair[b][:, 0, :], g_sb[b][:].indirect(nxt_sb[0][:]), gate2_sb[:, 0, :], MULT)
            nc.scalar.activation(plain[b][:], g_sb[b][:].indirect(nxt_sb[1][:]), ACT.Copy)
        for b in range(G_TILES):
            nc.vector.tensor_tensor(pair[b][:, 1, :], plain[b][:], gate2_sb[:, 1, :], MULT)
        for b in range(G_TILES):
            nc.vector.tensor_tensor(result[b][:], pair[b][:, 0, :], pair[b][:, 1, :], ADD)
            nc.sync.dma_start(out[b * P : (b + 1) * P, :], result[b][:])
